import numpy as np, ml_dtypes
CORES = [3,7,11,15,131,135,139,143]
N = 8
import mx_ref
BF = ml_dtypes.bfloat16
def gentries(a):
    return np.ascontiguousarray(a.reshape(8, 16, -1).transpose(0, 2, 1)).reshape(8, -1)
def gtable(e):
    e = np.asarray(e); return np.ascontiguousarray(e.reshape(8, -1, 16).transpose(0, 2, 1)).reshape(128, -1).astype(np.int32)
def gcols(t, e):
    v = np.concatenate([t.reshape(8, 16, -1, 4), np.zeros((8, 16, 1, 4), BF)], axis=2)
    return np.ascontiguousarray(np.stack([v[g][:, e[g]] for g in range(8)])).reshape(128, -1)
def tile(rs):
    return np.stack(rs, axis=2).reshape(128, -1).astype(BF)
def pick(q, e):
    c = np.concatenate([q[0].reshape(128, -1, 4), np.zeros((128, 1, 4), np.uint8)], axis=1); s = np.concatenate([q[1], np.ones((16, 1), np.uint8)], axis=1)
    return (np.ascontiguousarray(c[:, e].reshape(128, -1)), np.ascontiguousarray(s[:, e]))
def join(*qs):
    return (np.concatenate([q[0] for q in qs], axis=1), np.concatenate([q[1] for q in qs], axis=1))
def put(q, e, v):
    c, s = q[0].reshape(128, -1, 4).copy(), q[1].copy(); c[:, e] = v[0].reshape(128, -1, 4); s[:, e] = v[1]
    return (c.reshape(128, -1), s)
def pk(c, s):
    return (np.ascontiguousarray(c), mx_ref.live(s))
def emit(q):
    return q[0], q[1]
def packed(v, rng):
    q = [mx_ref.quantize(np.ascontiguousarray(v[r])) for r in range(N)]
    return np.stack([a for a, b in q]), np.stack([mx_ref.plane(b, rng) for a, b in q])
def values_of_codes():
    e, c = np.zeros((128, 128, 4), np.float32), np.zeros((128, 2, 4), np.uint8)
    e[np.arange(128), np.arange(128), 0] = 1
    c[:127, :, 0] = np.arange(256).reshape(2, 128).T[:127]
    return mx_ref.matmul(mx_ref.quantize(e.reshape(128, 512).astype(BF)), (c.reshape(128, 8), np.full((16, 2), 127, np.uint8))).T.reshape(-1).astype(np.float64)
CODE_VALUE, SCALE_VALUE = values_of_codes(), 2.0 ** (np.arange(256) - 127.0)
def decode(q):
    return (CODE_VALUE[q[0]].reshape(16, 8, -1, 4) * SCALE_VALUE[q[1]][:, None, :, None] + 0.0).reshape(128, -1).astype(np.float32)
def f(rng, *shape):
    return mx_ref.flush((rng.standard_normal(shape, dtype=np.float32) * np.exp2(rng.integers(-2, 3, shape[:-1] + (1,)))).astype(BF))
def wide(rng, *shape, cols=0):
    v = rng.standard_normal(shape, dtype=np.float32) * np.exp2(rng.integers(-12, 13, shape)).astype(np.float32)
    if cols: v *= np.repeat(np.exp2(rng.integers(-cols, cols + 1, shape[:-2] + (1, shape[-1] // 4))) * (rng.random(shape[:-2] + (1, shape[-1] // 4)) > 0.0625), 4, axis=-1).astype(np.float32)
    return mx_ref.flush(v.astype(BF))
C, H, E, R = 288, 96, 384, 3
def big(v):
    v = v.astype(np.float32)
    v[np.abs(v) < np.float32(2.0 ** -16)] = 0
    return v.astype(BF)
def numbers_of(rng):
    return {"x": big(f(rng, N, 128, 4 * C)), "u": np.array(f(rng, N, 128, 512)), "v": np.array(f(rng, N, 128, 512))}
def stored(a):
    return np.stack([gtable(a[r]) for r in range(N)])
def lists(rng):
    return {"lf": stored(rng.integers(0, E, (N, 8, E))), "rt": stored(rng.integers(0, E, (N, 8, E)))}
def layers(rng, still=[]):
    w = big(f(rng, N, 128, 2048)).reshape(N, 8, 16, 4, 8, 16, 4)
    for i in still:
        w[:, :, i] = 0
        w[:, :, :, :, :, i] = 0
    return w
def weights(rng, w):
    c, p = packed(np.ascontiguousarray(w).reshape(N, 128, 2048), rng)
    return {"wc": c, "ws": p}
def setup_inputs(rng):
    return {**numbers_of(rng), **lists(rng), **weights(rng, layers(rng))}
def setup_inputs_ties(rng):
    d = numbers_of(rng)
    o = rng.permutation(N)
    x = d["x"].reshape(N, 8, 16, C, 4)
    x[:, :, 0] = 0
    x[:, :, 0, :, 0] = rng.integers(-2, 3, (N, 8, C)).astype(np.float32).astype(BF)
    u = d["u"].reshape(N, 128, 128, 4)
    u[:, :, ::16] = 0
    for h in range(0, 128, 16): u[:, h, h, 0] = 1
    u[o[0], :, ::16] = 0
    e = lists(rng)
    e["rt"][o[1]] = e["lf"][o[1]]
    return {"x": x.reshape(N, 128, 4 * C), "u": u.reshape(N, 128, 512), "v": d["v"], **e, **weights(rng, layers(rng, [0]))}
def setup_inputs_near(rng):
    d = numbers_of(rng)
    kind = rng.permutation(8) % 4
    x = d["x"].astype(np.float32).reshape(N, 8, 16, C, 4)
    c = rng.integers(0, 2, (N, 8, C)) * 2.0 - 1.0
    s = rng.integers(0, 16, (N, 8, C))
    x[:, :, 0] = 0
    x[:, :, 8:] = 0
    x[:, :, 0, :, 0] = c
    x[:, :, 8] = c[:, :, :, None] * ((s[:, :, :, None] >> np.arange(4)) & 1) * np.exp2(np.arange(4) - 23.0)
    x[:, :, 11, :, 0] = c * 2.0 ** -10
    u = d["u"].reshape(N, 128, 128, 4)
    u[:, :, ::16] = 0
    for g in range(8):
        h, m = 16 * g, 1.0 if kind[g] == 0 else 2.0 ** -30
        if kind[g] < 2:
            u[:, h, h, 0] = m
            u[:, h + 11, h, 0] = m
        if kind[g] < 3: u[:, h + 8, h] = m
        else:
            a = rng.integers(0, 2, (N, C))
            x[:, g, 8:] = 0
            x[:, g, 10, :, 0] = c[:, g] * a * 1.125 * 2.0 ** -30
            x[:, g, 10, :, 1] = c[:, g] * (1 - a) * 1.25 * 2.0 ** -30
            u[:, h + 10, h, 0] = m * 1.125
            u[:, h + 10, h, 1] = m
    x = (x + np.float32(0.0)).reshape(N, 128, 4 * C).astype(BF)
    return {"x": x, "u": u.reshape(N, 128, 512), "v": d["v"], **lists(rng), **weights(rng, layers(rng, [0, 8, 9, 10, 11, 12, 13, 14, 15]))}
def setup_inputs_twice(rng):
    d = numbers_of(rng)
    x = (2 * rng.integers(0, 8, (N, 8, 16, C, 4)) + 1) * np.exp2(rng.integers(-17, -15, (N, 8, 16, C, 4))) * (rng.integers(0, 2, (N, 8, 16, C, 4)) * 2.0 - 1.0)
    x[:, :, ::8, :, 0] = np.where(rng.random((N, 8, 2, C)) < 0.5, 1.96875, 1.75) * (rng.integers(0, 2, (N, 8, 2, C)) * 2.0 - 1.0)
    a = int(rng.integers(1, 8))
    x[:, a, ::8, :, 0] = 1.75
    t = np.arange(C) % 4 == rng.integers(0, 4, (N, 1))
    x[:, 0] = np.where(t[:, None, :, None], 0.0, x[:, 0])
    x[:, 0, ::8, :, 0] = np.where(t[:, None], 1.75 * 2.0 ** -24 * (rng.integers(0, 2, (N, 2, C)) * 2.0 - 1.0), x[:, 0, ::8, :, 0])
    u = d["u"].reshape(N, 128, 128, 4)
    u[:, ::8, ::16] = 0
    w = np.zeros((N, 128, 4, 128, 4), np.float32)
    i = np.arange(128)
    for b in range(4): w[:, i, b, i, b] = -32
    w[:, i[::16], 0, i[::16], 0] = -36
    w[:, i[8::16], 0, i[8::16], 0] = -18
    w[:, :, :, :16] = 0
    w[:, :, :, 16 * a:16 * a + 16] = 0
    m = np.arange(16)
    k = np.where(np.arange(N) % 2 == rng.integers(0, 2), 1.0, -1.0)[:, None]
    for b in range(4): w[:, 16 * a + m, b, m, b] = 32 * k
    w[:, 16 * a + m[::8], 0, m[::8], 0] = 36 * k
    e = rng.integers(0, E, (2, N, 8, E))
    for r in range(N):
        e[:, r, 0, :C] = rng.permutation(np.concatenate([np.arange(H), np.arange(C, E), H + rng.permutation(C - H)[:C - 2 * H]]))
    return {"x": x.astype(np.float32).reshape(N, 128, 4 * C).astype(BF), "u": u.reshape(N, 128, 512), "v": d["v"], "lf": stored(e[0]), "rt": stored(e[1]), **weights(rng, w.astype(BF))}
def setup_inputs_ends(rng):
    d = numbers_of(rng)
    e = rng.permutation(N)
    h = rng.permutation(8)
    most = 1.34375 * 2.0 ** 28
    x = (0.6 + 0.4 * rng.random((N, 8, 16, C, 4))) * most
    x[e[::2]] = most
    c = rng.integers(0, 2, (N, 1, 1, C, 1)) * 2.0 - 1.0
    c[e[1]] = c[e[1], 0, 0, 0, 0]
    x = x * c
    x[:, h[4:], 8:] = (rng.integers(0, 2, (N, 4, 8, C, 4)) * 2.0 - 1.0) * 2.0 ** -30
    u = d["u"].reshape(N, 128, 128, 4)
    u[:, :, ::16] = 0
    for g in h[:4]: u[:, :, 16 * g] = (2.0 ** 30 * (1.0 - 0.1 * rng.random((N, 128, 4))) * rng.choice([-1.0, 1.0], (N, 1, 1))).astype(np.float32).astype(BF)
    for g in h[4:]: u[:, 16 * g + 8:16 * g + 16, 16 * g] = 2.0 ** -30
    u[e[2], :, ::16] = 0
    v = d["v"]
    v[e[:2]] = (2.0 ** 30 * rng.choice([-1.0, 1.0], (2, 128, 512))).astype(np.float32).astype(BF)
    a = rng.integers(0, 2, (2, N, 8, E)) * (E - 1)
    a[:, e[0]] = E - 1
    a[:, e[1]] = 0
    a[:, e[2]] = np.argsort(rng.random((2, 8, E)), axis=2)
    p, m = np.arange(C), rng.permutation(C)
    for g, k in enumerate(rng.permutation(8)):
        t = rng.permutation(E)
        if k == 0: t = np.concatenate([rng.permutation(C), C + rng.permutation(H)])
        elif H * (k - 1) < C: t = np.concatenate([C + rng.permutation(H), rng.permutation(C)])
        a[0, e[2], g, np.concatenate([p[np.roll(m, -H * (k - 1))], np.setdiff1d(np.arange(E), p)])] = t
        p = a[0, e[2], g, p]
    a[:, e[3]] = rng.integers(0, C, (2, 8, E))
    w = np.zeros((N, 128, 4, 128, 4), np.float32)
    i = np.flatnonzero(np.arange(128) % 16 < 8)
    k = rng.choice([-4.0, 4.0], (N, 1))
    for b in range(4): w[:, i, b, i, b] = k
    v = (np.where(v < 0, -1.0, 1.0) * np.where(rng.permutation(N) % 2, 2.0 ** -30, 2.0 ** 30)[:, None, None]).astype(np.float32).astype(BF)
    return {"x": x.astype(np.float32).reshape(N, 128, 4 * C).astype(BF), "u": u.reshape(N, 128, 512), "v": v, "lf": stored(a[0]), "rt": stored(a[1]), **weights(rng, w.astype(BF))}
def setup_inputs_spread(rng):
    d = numbers_of(rng)
    w = (layers(rng).astype(np.float32) * np.float32(0.125)).astype(BF)
    return {"x": big(wide(rng, N, 128, 4 * C, cols=4)), "u": d["u"], "v": d["v"], **lists(rng), **weights(rng, w)}
def check_inputs(d):
    b = []
    for k in ("x", "u", "v"):
        a = np.abs(d[k].astype(np.float32))
        if not (np.isfinite(a).all() and ((a == 0) | (a >= 2.0 ** -30) & (a <= 2.0 ** 30)).all()): b.append("a value of " + k)
    for k in ("lf", "rt"):
        if not ((d[k] >= 0) & (d[k] < E)).all(): b.append("an entry of " + k)
    none, least, most = [emit(mx_ref.quantize(np.full((128, 16), k, np.float32).astype(BF)))[1][0, 0] for k in (0.0, 2.0 ** -30, 2.0 ** 30)]
    size = 0.0
    for r in range(N):
        if ((d["wc"][r] == 0x7F) | (d["wc"][r] == 0xFF)).any(): b.append("wc: a code that is no number")
        s = mx_ref.live(d["ws"][r])
        if ((s != none) & ((s < least) | (s > most))).any(): b.append("ws: a scale out of range")
        full = ((d["wc"][r] & 0x7F) != 0).reshape(16, 8, 512, 4).any(axis=(1, 3))
        if (full & (s == none)).any(): b.append("wc: a code other than zero at the scale of zeros")
        with np.errstate(all="ignore"):
            size = np.maximum(size, np.max(np.sum(np.abs(decode(pk(d["wc"][r], d["ws"][r])).astype(np.float64)).reshape(128, 512, 4), axis=(0, 2))))
    with np.errstate(all="ignore"):
        if not np.max(np.abs(d["x"].astype(np.float64))) * (1.125 + 2.5 * size * 2.0 ** -5) ** 3 <= 2.0 ** 30: b.append("the sizes of x and W together")
    return b
def reference(x, u, v, lf, rt, wc, ws):
    qu = [mx_ref.quantize(u[r]) for r in range(N)]
    lay = [pk(wc[r], ws[r]) for r in range(N)]
    left = [gentries(lf[r]) for r in range(N)]
    right = [gentries(rt[r]) for r in range(N)]
    now = [x[r] for r in range(N)]
    took = np.zeros((N, 8, C), np.int64)
    for t in range(R):
        q = [mx_ref.quantize(now[r]) for r in range(N)]
        edge = [pick(q[r], np.arange(H)) for r in range(N)]
        own = [decode(q[r]) for r in range(N)]
        flux, back = [], []
        for r in range(N):
            e = (r + 1) % N
            s = np.abs(mx_ref.matmul(qu[r], join(q[r], edge[e]))[::16])
            l, k = np.arange(C), np.arange(C)
            for g in range(8):
                a, b = left[r][g, l], right[r][g, k]
                first = s[g, a] <= s[g, b]
                took[r, g] = np.where(first, a, b)
                l, k = np.where(first, a, l), np.where(first, k, b)
            window = np.concatenate([own[r], own[e][:, :4 * H]], axis=1).astype(BF)
            z = mx_ref.quantize(gcols(window, took[r]))
            h = mx_ref.quantize(tile([mx_ref.matmul(pick(lay[r], np.arange(128 * b, 128 * b + 128)), z) * np.float32(0.03125) for b in range(4)]))
            c = np.full((8, E), -1)
            for g in range(8):
                i, j = np.unique(took[r, g], return_index=True)
                c[g, i] = j
            w = gcols(decode(h).astype(BF), c)
            flux.append(w[:, :4 * C].astype(np.float32))
            back.append(decode(mx_ref.quantize(np.ascontiguousarray(w[:, 4 * C:]))))
        for r in range(N):
            n = own[r] - flux[r]
            n[:, :4 * H] = n[:, :4 * H] - back[(r - 1) % N]
            now[r] = n.astype(BF)
    y, on = np.zeros((N, 128, C), np.float32), np.zeros((N, 8, C), np.float32)
    oc, osc = np.zeros((N, 128, 4 * C), np.uint8), np.zeros((N, 16, C), np.uint8)
    for r in range(N):
        q = mx_ref.quantize(now[r])
        y[r] = mx_ref.matmul(mx_ref.quantize(v[r]), q)
        on[r] = took[r]
        oc[r], osc[r] = emit(q)
    return {"y": y, "on": on, "oc": oc, "osc": osc}

@@ -1,0 +1,304 @@
+from concourse.mybir import dt, AluOpType as A, ActivationFunctionType as F
+
+C, H, E, R, N = 288, 96, 384, 3, 8
+BIG = 1e29
+SCRATCH = {"pp": ("psum", [128, 4096], "float32")}
+for names, w in (("qx", 480), ("uq", 128), ("ur", 1024), ("vq", 128), ("wq", 512), ("eq", 512), ("mq", 288), ("tq", 288), ("bq", 128)):
+    SCRATCH[names] = ("sbuf", [128, w], "float8_e4m3fn_x4")
+    SCRATCH[names + "s"] = ("sbuf", [128, w], "uint8")
+for names, w, d in (("x0 xt mt tt uo", 1152, "bfloat16"), ("ut vt ub", 512, "bfloat16"), ("eb", 528, "bfloat16"), ("vp", 1536, "bfloat16"), ("dp", 1216, "bfloat16"),
+                    ("si md rst inm ins xf", 384, "float32"), ("idt inv", 400, "float32"), ("mk1 mki", 96, "float32"),
+                    ("mk2 nf nx ny ne nz no yo", 288, "float32"), ("rc rd r2", 4, "float32"), ("lk0 ab0", 6, "float32"), ("lrf", 768, "float32"),
+                    ("tb", 6144, "float32"), ("sw", 3072, "float32"), ("n8", 24, "float32"), ("off dm dn", 18, "float32"),
+                    ("gs_0 gs_1 xg_0 xg_1 xs_0 xs_1", 96, "float32"), ("cm_0 cm_1 cs_0 cs_1", 48, "float32"), ("dd_0 dd_1", 9, "float32"),
+                    ("bb_0 bb_1", 3, "float32"), ("mm_0 mm_1 lk_0 lk_1", 6, "float32"),
+                    ("pi ri", 4, "int32"), ("ji", 3, "int32"), ("uli", 64, "int32"), ("lri", 48, "int32"), ("ab0i", 6, "int32"),
+                    ("ul", 64, "uint16"), ("lru", 48, "uint16"), ("oa0 oa_0 oa_1 lu_0 lu_1", 6, "uint16"), ("nu", 18, "uint16"), ("du", 36, "uint16"), ("iu", 24, "uint16")):
+    for name in names.split():
+        SCRATCH[name] = ("sbuf", [128, w], d)
+SEMAPHORES = "sv st sa sg dx dx2 dl da du dw dv dn brd bl ret rl do dp".split() + ["dt%d" % k for k in range(8)]
+B4 = range(4)
+
+
+def rank_program(g, core, T, topo):
+    rank = T.rank_of(core)
+    if rank is None:
+        return
+    nxt, prv = T.cores[(rank + 1) % N], T.cores[(rank - 1) % N]
+    V, P, S = g.vector, g.tensor, g.scalar
+    eng = {"v": V, "t": P, "s": S, "g": g, "y": g.sync}
+    own = {"v": "sv", "t": "st", "s": "sa", "g": "sg"}
+    total = {n: 0 for n in SEMAPHORES}
+    know = {q: {} for q in eng}
+    snaps = {n: [] for n in SEMAPHORES}
+    wr, rd = {}, {}
+
+    def learn(q, sem, val):
+        k = know[q]
+        if k.get(sem, 0) >= val:
+            return
+        eng[q].wait_ge(T.sem[sem], val)
+        k[sem] = val
+        for v, s in snaps[sem]:
+            if v <= val:
+                for a, b in s.items():
+                    k[a] = max(k.get(a, 0), b)
+
+    def need(q, reads, writes):
+        w = {}
+        l = [r for key in list(reads) + list(writes) for r in wr.get(key, [])]
+        l += [r for key in writes for r in rd.get(key, []) if r[3] or r[0] != q]
+        for oq, sem, val, d in l:
+            if know[q].get(sem, 0) < val:
+                w[sem] = max(w.get(sem, 0), total[sem] if d else val)
+        for sem in w:
+            learn(q, sem, w[sem])
+
+    def done(q, sem, inc, reads, writes, d, more=False):
+        total[sem] += inc
+        snaps[sem].append((total[sem], dict(know[q])))
+        rec = (q, sem, total[sem], d)
+        for key in writes:
+            wr[key] = (wr.get(key, []) if more else []) + [rec]
+            if not more:
+                rd[key] = []
+        for key in reads:
+            rd.setdefault(key, []).append(rec)
+
+    def op(q, f, reads, writes, *a, **kw):
+        need(q, reads, writes)
+        f(*a, **kw).then_inc(T.sem[own[q]], 1)
+        done(q, own[q], 1, reads, writes, False)
+
+    def dma(q, sem, out, in_, reads, writes, more=True):
+        need(q, reads, [] if more else writes)
+        eng[q].dma_start(out, in_).then_inc(T.sem[sem], 16)
+        done(q, sem, 16, reads, writes, True, more)
+
+    def send(dst, rsem, lsem, q, d0, s, s0, reads):
+        need("g", reads, [])
+        rid, pid = topo.addr(dst, core)
+        for o, i in ((T[q][:, d0:d0 + H].bitcast(dt.uint8), T[s][:, s0:s0 + H].bitcast(dt.uint8)), (T[q + "s"][:, d0:d0 + H], T[s + "s"][:, s0:s0 + H])):
+            g.remote_dma(o, i, T.sem[rsem], T.sem[lsem], pid, rid, topo.mask(core, dst))
+            done("g", lsem, len(topo.engines(core, dst)), reads, [], True)
+
+    def arrive(rsem, src, key):
+        total[rsem] += 2 * len(topo.engines(src, core))
+        wr[key], rd[key] = [("r", rsem, total[rsem], True)], []
+
+    def bank(k, n=C, a=0):
+        return T.pp[:, 512 * k + a:512 * k + a + n]
+
+    def mm(k, n, l, l0, r, r0, reads):
+        op("t", P.matmul_mx, reads, ["pb%d" % k], bank(k, n), T[l][:, l0:l0 + 128], T[l + "s"][:, l0:l0 + 128], T[r][:, r0:r0 + n], T[r + "s"][:, r0:r0 + n], True, True)
+
+    def act(out, in_, func, reads, writes, **kw):
+        op("s", S.activation, reads, writes, out, in_, func, **kw)
+
+    def tt(out, a, b, o, reads, writes):
+        op("v", V.tensor_tensor, reads, writes, out, a, b, o)
+
+    def ts(reads, writes, *a):
+        op("v", V.tensor_scalar, reads, writes, *a)
+
+    def cp(out, a, reads, writes):
+        op("v", V.tensor_copy, reads, writes, out, a)
+
+    def fill(out, c, writes):
+        op("v", V.memset, [], writes, out, c)
+
+    def scan(out, d1, n, reads, writes):
+        op("v", V.tensor_tensor_scan, ["rst"] + reads, writes, out, T.rst[:, 0:n], d1, 0.0, A.mult, A.add)
+
+    def quant(q, a, b, tile, t0, reads, writes):
+        op("v", V.quantize_mx, reads, writes, T[q][:, a:b], T[q + "s"][:, a:b], T[tile][:, t0:t0 + 4 * (b - a)])
+
+    def iota(n, pattern, cm, **kw):
+        op("g", g.iota, [], [n], T[n][:], pattern, 0, cm, **kw)
+
+    def each(s):
+        return [s % b for b in B4]
+
+    def send_border():
+        send(prv, "brd", "bl", "qx", 384, "qx", 96, ["qa"])
+        arrive("brd", nxt, "qr")
+
+    dma("y", "dx", T.x0[:, 0:512], T.x[:, 0:512], [], ["x0a"])
+    dma("s", "dl", T.lri[:, 0:24], T.lf[:], [], ["lri"])
+    dma("s", "dl", T.lri[:, 24:48], T.rt[:], [], ["lri"])
+    dma("y", "dx2", T.x0[:, 512:1152], T.x[:, 512:1152], [], ["x0b"])
+    dma("s", "du", T.ut[:], T.u[:], [], ["ut"])
+    for h in range(8):
+        c = 3 * h if h < 6 else 0
+        dma("y", "da", T.ab0i[16 * h:16 * h + 16, 0:3], T.lf[0:16, c:c + 3], [], ["ab0i"])
+        dma("y", "da", T.ab0i[16 * h:16 * h + 16, 3:6], T.rt[0:16, c:c + 3], [], ["ab0i"])
+    iota("pi", [[0, 4]], 1)
+    iota("uli", [[16, 8], [0, 8]], 0)
+    iota("ji", [[16, 3]], 3)
+    iota("si", [[0, 24], [1, 16]], 0, allow_small_or_imprecise_dtypes=True)
+    iota("idt", [[1, 400]], 0, allow_small_or_imprecise_dtypes=True)
+    fill(T.eb[:], 1.0, ["eb"])
+    fill(T.ub[:, 384:512], 0.0, ["ubz"])
+    for b in B4:
+        fill(T.dp[:, 304 * b + 288:304 * b + 304], 0.0, ["dpz%d" % b])
+    fill(T.mk1[:, 0:48], BIG, ["mk1a"])
+    fill(T.nx[:], 0.0, ["nx"])
+    cp(T.ul[:], T.uli[:], ["uli"], ["ul"])
+    ts(["pi"], ["ri"], T.ri[:], T.pi[:], 15, None, A.bitwise_and)
+    cp(T.rc[:], T.ri[:], ["ri"], ["rc"])
+    ts(["rc"], ["rd"], T.rd[:], T.rc[:], 384.0, None, A.add)
+    ts(["rc"], ["r2"], T.r2[:], T.rc[:], -2.0, None, A.mult)
+    ts(["ji", "r2"], ["lk0a"], T.lk0[:, 0:3], T.ji[:], T.r2[:, 0:1], None, A.add)
+    ts(["lk0a"], ["lk0b"], T.lk0[:, 3:6], T.lk0[:, 0:3], 384.0, None, A.add)
+    quant("qx", 96, 224, "x0", 0, ["x0a"], ["qa"])
+    send_border()
+    op("g", g.affine_select, ["eb"], ["eb"], T.eb[:], T.eb[:], [[1, 528]], A.is_equal, 0.0, -3, -4)
+    quant("qx", 224, 384, "x0", 512, ["x0b"], ["qb"])
+    cp(T.lru[:], T.lri[:], ["lri"], ["lru"])
+    cp(T.lrf[:, 0:384], T.idt[:, 0:400].indirect(T.lru[:, 0:24]), ["lru", "idt"], ["lrfa"])
+    act(T.lrf[:, 384:768], T.idt[:, 0:400].indirect(T.lru[:, 24:48]), F.Copy, ["lru", "idt"], ["lrfb"])
+    for k in range(1, 8):
+        for h in range(8):
+            dma("y", "dt%d" % k, T.tb[16 * h:16 * h + 16, 768 * k:768 * k + 768], T.lrf[16 * k:16 * k + 16, :], ["lrfa", "lrfb"], ["tb%d" % k])
+    quant("uq", 0, 128, "ut", 0, ["ut"], ["uq"])
+    cp(T.ur[:, 0:1024].bitcast(dt.uint32), T.uq[:, 0:128].bitcast(dt.uint32).indirect(T.ul[:, 0:64]), ["uq", "ul"], ["ur"])
+    act(T.urs[:, 0:1024], T.uqs[:, 0:128].indirect(T.ul[:, 0:64]), F.Copy, ["uq", "ul"], ["urs"])
+    for b in B4:
+        quant("eq", 128 * b, 128 * b + 128, "eb", 3 - b, ["eb"], ["eq%d" % b])
+    ts(["si", "rc"], ["md"], T.md[:], T.si[:], T.rc[:, 0:1], None, A.is_equal)
+    ts(["si"], ["rst"], T.rst[:], T.si[:], 0.0, None, A.is_gt)
+    ts(["md"], ["mk1b"], T.mk1[:, 48:96], T.md[:, 0:48], BIG, -1.0, A.mult, A.add)
+    ts(["md"], ["mki"], T.mki[:], T.md[:, 0:96], 1000000.0, None, A.mult)
+    ts(["si", "rc"], ["mk2"], T.mk2[:], T.si[:, 0:288], T.rc[:, 0:1], 1000000.0, A.is_lt, A.mult)
+    ts(["mk2"], ["mk2"], T.mk2[:], T.mk2[:], -1.0, None, A.add)
+    cp(T.ab0[:], T.ab0i[:], ["ab0i"], ["ab0"])
+    cp(T.oa0[:], T.ab0i[:], ["ab0i"], ["oa0"])
+    dma("s", "dw", T.wq[:].bitcast(dt.uint8), T.wc[:], [], ["wq"])
+    dma("s", "dw", T.wqs[:], T.ws[:], [], ["wq"])
+    dma("s", "dv", T.vt[:], T.v[:], [], ["vt"])
+
+    for t in range(R):
+        for k in range(8):
+            mm(k, C, "ur", 128 * k, "qx", 96, ["ur", "urs", "qa", "qb"])
+            act(T.sw[:, 384 * k:384 * k + 288], bank(k), F.Abs, ["pb%d" % k], ["sw%da" % k])
+        for b in B4:
+            mm(b, C, "eq", 128 * b, "qx", 96, ["eq%d" % b, "qa", "qb"])
+            cp(T.vp[:, 384 * b:384 * b + 288], bank(b), ["pb%d" % b], ["vp%da" % b])
+        for k in range(8):
+            mm(k, 128, "ur", 128 * k, "qx", 352, ["ur", "urs", "qb", "qr"])
+            act(T.sw[:, 384 * k + 288:384 * k + 384], bank(k, 96, 32), F.Abs, ["pb%d" % k], ["sw%db" % k])
+        for b in B4:
+            mm(b, 128, "eq", 128 * b, "qx", 352, ["eq%d" % b, "qb", "qr"])
+        for k in range(8):
+            z, zp = "_%d" % (k % 2), "_%d" % (1 - k % 2)
+            if k == 0:
+                src, o, ak, oa, oak, lk, la, lb = T.ab0, [0, 3, 1], "ab0", T.oa0, "oa0", T.lk0, "lk0a", "lk0b"
+            else:
+                src, o, ak, oa, oak, lk, la, lb = T["xs" + zp], [15, 63, 16], "xs" + zp, T["oa" + z], "oa" + z, T["lk" + zp], "lka" + zp, "lkb" + zp
+                cp(oa[:], src[:, 15:96:16], [ak], [oak])
+            a, b = src[:, o[0]:o[0] + 2 * o[2] + 1:o[2]], src[:, o[1]:o[1] + 2 * o[2] + 1:o[2]]
+            gs, cm, cs, dd, bb, m2, ln, lu, xg = [T[n + z] for n in "gs cm cs dd bb mm lk lu xg".split()]
+            tt(gs[:], T.sw[:, 384 * k:384 * k + 384].indirect(oa[:, 0:6]), T.mk1[:], A.min, [oak, "sw%da" % k, "sw%db" % k, "mk1a", "mk1b"], ["gs" + z])
+            if k < 7:
+                ts([ak], ["bb" + z], bb[:], b, 384.0, None, A.add)
+                tt(dd[:, 0:3], a, lk[:, 0:3], A.subtract, [ak, la], ["da" + z])
+            tt(dd[:, 6:9], a, b, A.subtract, [ak], ["dc" + z])
+            if k < 7:
+                tt(dd[:, 3:6], lk[:, 3:6], bb[:], A.subtract, ["bb" + z, lb], ["db" + z])
+            tt(cm[:], gs[:, 0:48], gs[:, 48:96], A.is_le, ["gs" + z], ["cm" + z])
+            scan(cs[:], cm[:], 48, ["cm" + z], ["cs" + z])
+            c = cs[:, 15:48:16]
+            if k < 7:
+                tt(m2[:, 0:3], c, dd[:, 0:3], A.mult, ["cs" + z, "da" + z], ["ma" + z])
+                tt(m2[:, 3:6], c, dd[:, 3:6], A.mult, ["cs" + z, "db" + z], ["mb" + z])
+                tt(ln[:, 0:3], m2[:, 0:3], lk[:, 0:3], A.add, ["ma" + z, la], ["lka" + z])
+                tt(ln[:, 3:6], m2[:, 3:6], bb[:], A.add, ["mb" + z, "bb" + z], ["lkb" + z])
+                cp(lu[:], ln[:], ["lka" + z, "lkb" + z], ["lu" + z])
+                tt(xg[:], T.tb[:, 768 * k + 768:768 * k + 1536].indirect(lu[:, 0:6]), T.mki[:], A.min, ["lu" + z, "tb%d" % (k + 1), "mki"], ["xg" + z])
+                scan(T["xs" + z][:], xg[:], 96, ["xg" + z], ["xs" + z])
+                for q in range(3):
+                    act(T.n8[:, 3 * k + q:3 * k + q + 1], cs[:, 16 * q + 15:16 * q + 16], F.Identity, ["cs" + z, "dc" + z, ak], ["n8%d_%d" % (k, q)],
+                        bias=src[:, o[1] + o[2] * q:o[1] + o[2] * q + 1], scale=dd[:, 6 + q:7 + q])
+            else:
+                tt(m2[:, 0:3], c, dd[:, 6:9], A.mult, ["cs" + z, "dc" + z], ["ma" + z])
+                tt(T.n8[:, 21:24], m2[:, 0:3], b, A.add, ["ma" + z, ak], ["n87_%d" % q for q in range(3)])
+            if k == 3:
+                for b2 in B4:
+                    act(T.vp[:, 384 * b2 + 288:384 * b2 + 384], bank(b2, 96, 32), F.Copy, ["pb%d" % b2], ["vp%db" % b2])
+            if k == 0:
+                need("y", [], ["off"])
+                wr["off"], rd["off"] = [], []
+            for h in range(6):
+                dma("y", "dn", T.off[16 * k:16 * k + 16, 3 * h:3 * h + 3], T.n8[16 * h:16 * h + 16, 3 * k:3 * k + 3], ["n8%d_%d" % (k, q) for q in range(3)], ["off"])
+        fill(T.inv[:], 288.0, ["inv"])
+        cp(T.nu[:], T.off[:], ["off"], ["nu"])
+        for b in B4:
+            w, rds = T.vp[:, 384 * b:384 * b + 384].indirect(T.nu[:, 0:18]), ["nu", "vp%da" % b, "vp%db" % b]
+            if b < 2:
+                act(T.mt[:, b:1152:4], w, F.Copy, rds, ["mt%d" % b])
+            else:
+                cp(T.mt[:, b:1152:4], w, rds, ["mt%d" % b])
+        quant("mq", 0, 288, "mt", 0, each("mt%d"), ["mq"])
+        for b in B4:
+            mm(b, C, "wq", 128 * b, "mq", 0, ["wq", "mq"])
+            act(T.tt[:, b:1152:4], bank(b), F.Copy, ["pb%d" % b], ["tt%d" % b], scale=0.03125)
+        for b in B4:
+            mm(4 + b, C, "eq", 128 * b, "qx", 96, ["eq%d" % b, "qa", "qb"])
+        tt(T.nf[:], T.idt[:, 0:400].indirect(T.nu[:, 0:18]), T.mk2[:], A.min, ["idt", "nu", "mk2"], ["nf"])
+        cp(T.nx[:, 0:288:16], T.off[:], ["off"], ["nx"])
+        scan(T.ny[:], T.nx[:], 288, ["nx"], ["ny"])
+        tt(T.ne[:], T.nf[:], T.ny[:], A.is_equal, ["nf", "ny"], ["ne"])
+        scan(T.nz[:], T.ne[:], 288, ["ne"], ["nz"])
+        ts(["nz", "rd"], ["dm"], T.dm[:], T.nz[:, 15:288:16], 0.0, T.rd[:, 0:1], A.is_gt, A.mult)
+        tt(T.dn[:], T.dm[:], T.off[:], A.max, ["dm", "off"], ["dn"])
+        cp(T.du[:, 0:36:2], T.dn[:], ["dn"], ["du"])
+        quant("tq", 0, 288, "tt", 0, each("tt%d"), ["tq"])
+        for b in B4:
+            mm(b, C, "eq", 128 * b, "tq", 0, ["eq%d" % b, "tq"])
+            act(T.dp[:, 304 * b:304 * b + 288], bank(b), F.Copy, ["pb%d" % b], ["dp%d" % b])
+        for q in range(17, -1, -1):
+            cp(T.inv[:, 0:400].indirect(T.du[:, 2 * q:2 * q + 1]), T.idt[:, 16 * q:16 * q + 16], ["du", "idt"], ["inv"])
+        for n, i, j in (("b", 288, 384), ("o", 0, 288)):
+            tt(T.inm[:, i:j], T.inv[:, i:j], T.md[:, i:j], A.mult, ["inv", "md"], ["inm" + n])
+            scan(T.ins[:, i:j], T.inm[:, i:j], j - i, ["inm" + n], ["ins" + n])
+            cp(T.iu[:, i // 16:j // 16], T.ins[:, i + 15:j:16], ["ins" + n], ["iu" + n])
+            if n == "b":
+                for b in B4:
+                    w, rds = T.dp[:, 304 * b:304 * b + 304].indirect(T.iu[:, 18:24]), ["iub", "dp%d" % b, "dpz%d" % b]
+                    if b < 2:
+                        act(T.ub[:, b:384:4], w, F.Copy, rds, ["ub%d" % b])
+                    else:
+                        cp(T.ub[:, b:384:4], w, rds, ["ub%d" % b])
+                quant("bq", 0, 128, "ub", 0, each("ub%d") + ["ubz"], ["bq"])
+                send(nxt, "ret", "rl", "qx", 0, "bq", 0, ["bq"])
+                arrive("ret", prv, "qt")
+        for b in B4:
+            w, rds, o = T.dp[:, 304 * b:304 * b + 304].indirect(T.iu[:, 0:18]), ["iuo", "dp%d" % b, "dpz%d" % b], T.uo[:, 288 * b:288 * b + 288]
+            if b % 2 == 0:
+                act(o, w, F.Copy, rds, ["uo%d" % b])
+            else:
+                cp(o, w, rds, ["uo%d" % b])
+        for b in (1, 0, 3, 2):
+            rds = ["pb%d" % (4 + b), "uo%d" % b]
+            tt(T.xf[:, 96 * b:96 * b + 96], bank(4 + b, 96), T.uo[:, 288 * b:288 * b + 96], A.subtract, rds, ["xf%d" % b])
+            tt(T.xt[:, 384 + b:1152:4], bank(4 + b, 192, 96), T.uo[:, 288 * b + 96:288 * b + 288], A.subtract, rds, ["xtb%d" % b])
+        quant("qx", 224, 384, "xt", 512, each("xtb%d"), ["qb"])
+        for b in B4:
+            mm(b, 128, "eq", 128 * b, "qx", 0, ["eq%d" % b, "qa", "qt"])
+            tt(T.xt[:, b:384:4], T.xf[:, 96 * b:96 * b + 96], bank(b, 96), A.subtract, ["xf%d" % b, "pb%d" % b], ["xta%d" % b])
+        quant("qx", 96, 224, "xt", 0, each("xta%d") + each("xtb%d"), ["qa"])
+        if t < R - 1:
+            send_border()
+    act(T.no[:], T.idt[:, 0:400].indirect(T.nu[:, 0:18]), F.Copy, ["nu", "idt"], ["no"])
+    quant("vq", 0, 128, "vt", 0, ["vt"], ["vq"])
+    for k in range(8):
+        dma("y", "do", T.on[k:k + 1, :], T.no[16 * k:16 * k + 1, :], ["no"], ["o"])
+    mm(0, C, "vq", 0, "qx", 96, ["vq", "qa", "qb"])
+    dma("y", "do", T.oc[:], T.qx[:, 96:384].bitcast(dt.uint8), ["qa", "qb"], ["o"])
+    for k in B4:
+        dma("y", "do", T.osc[4 * k:4 * k + 4, :], T.qxs[32 * k:32 * k + 4, 96:384], ["qa", "qb"], ["o"])
+    act(T.yo[:], bank(0), F.Copy, ["pb0"], ["yo"])
+    dma("s", "do", T.y[:], T.yo[:], ["yo"], ["o"])
+    for n in SEMAPHORES:
+        if total[n]:
+            learn("g", n, total[n])

@@ -7,11 +7,11 @@ for names, w in (("qx", 480), ("uq", 128), ("ur", 1024), ("vq", 128), ("wq", 512
     SCRATCH[names] = ("sbuf", [128, w], "float8_e4m3fn_x4")
     SCRATCH[names + "s"] = ("sbuf", [128, w], "uint8")
 for names, w, d in (("x0 xt mt tt uo", 1152, "bfloat16"), ("ut vt ub", 512, "bfloat16"), ("eb", 528, "bfloat16"), ("vp", 1536, "bfloat16"), ("dp", 1216, "bfloat16"),
-                    ("si md rst inm ins xf", 384, "float32"), ("idt inv", 400, "float32"), ("mk1 mki", 96, "float32"),
+                    ("si md rst inn inm ins xf", 384, "float32"), ("idt inv0 inv1", 400, "float32"), ("mk1 mki", 96, "float32"),
                     ("mk2 nf nx ny ne nz no yo", 288, "float32"), ("rc rd r2", 4, "float32"), ("lk0 ab0", 6, "float32"), ("lrf", 768, "float32"),
                     ("tb", 6144, "float32"), ("sw", 3072, "float32"), ("n8", 24, "float32"), ("off dm dn", 18, "float32"),
-                    ("gs_0 gs_1 xg_0 xg_1 xs_0 xs_1", 96, "float32"), ("cm_0 cm_1 cs_0 cs_1", 48, "float32"), ("dd_0 dd_1", 9, "float32"),
-                    ("bb_0 bb_1", 3, "float32"), ("mm_0 mm_1 lk_0 lk_1", 6, "float32"),
+                    ("gs_0 gs_1 xg_0 xg_1 xs_0 xs_1", 96, "float32"), ("cm_0 cm_1 cs_0 cs_1", 48, "float32"), ("dd_0 dd_1", 12, "float32"),
+                    ("lk_0 lk_1", 6, "float32"),
                     ("pi ri", 4, "int32"), ("ji", 3, "int32"), ("uli", 64, "int32"), ("lri", 48, "int32"), ("ab0i", 6, "int32"),
                     ("ul", 64, "uint16"), ("lru", 48, "uint16"), ("oa0 oa_0 oa_1 lu_0 lu_1", 6, "uint16"), ("nu", 18, "uint16"), ("du", 36, "uint16"), ("iu", 24, "uint16")):
     for name in names.split():
@@ -149,11 +149,10 @@ def rank_program(g, core, T, topo):
     ts(["rc"], ["rd"], T.rd[:], T.rc[:], 384.0, None, A.add)
     ts(["rc"], ["r2"], T.r2[:], T.rc[:], -2.0, None, A.mult)
     ts(["ji", "r2"], ["lk0a"], T.lk0[:, 0:3], T.ji[:], T.r2[:, 0:1], None, A.add)
-    ts(["lk0a"], ["lk0b"], T.lk0[:, 3:6], T.lk0[:, 0:3], 384.0, None, A.add)
+    ts(["ji", "r2"], ["lk0b"], T.lk0[:, 3:6], T.ji[:], T.r2[:, 0:1], None, A.add)
     quant("qx", 96, 224, "x0", 0, ["x0a"], ["qa"])
     send_border()
     op("g", g.affine_select, ["eb"], ["eb"], T.eb[:], T.eb[:], [[1, 528]], A.is_equal, 0.0, -3, -4)
-    quant("qx", 224, 384, "x0", 512, ["x0b"], ["qb"])
     cp(T.lru[:], T.lri[:], ["lri"], ["lru"])
     cp(T.lrf[:, 0:384], T.idt[:, 0:400].indirect(T.lru[:, 0:24]), ["lru", "idt"], ["lrfa"])
     act(T.lrf[:, 384:768], T.idt[:, 0:400].indirect(T.lru[:, 24:48]), F.Copy, ["lru", "idt"], ["lrfb"])
@@ -163,16 +162,17 @@ def rank_program(g, core, T, topo):
     quant("uq", 0, 128, "ut", 0, ["ut"], ["uq"])
     cp(T.ur[:, 0:1024].bitcast(dt.uint32), T.uq[:, 0:128].bitcast(dt.uint32).indirect(T.ul[:, 0:64]), ["uq", "ul"], ["ur"])
     act(T.urs[:, 0:1024], T.uqs[:, 0:128].indirect(T.ul[:, 0:64]), F.Copy, ["uq", "ul"], ["urs"])
-    for b in B4:
-        quant("eq", 128 * b, 128 * b + 128, "eb", 3 - b, ["eb"], ["eq%d" % b])
+    quant("qx", 224, 384, "x0", 512, ["x0b"], ["qb"])
     ts(["si", "rc"], ["md"], T.md[:], T.si[:], T.rc[:, 0:1], None, A.is_equal)
     ts(["si"], ["rst"], T.rst[:], T.si[:], 0.0, None, A.is_gt)
+    ts(["si", "rc"], ["mk2"], T.mk2[:], T.si[:, 0:288], T.rc[:, 0:1], 1000000.0, A.is_lt, A.mult)
     ts(["md"], ["mk1b"], T.mk1[:, 48:96], T.md[:, 0:48], BIG, -1.0, A.mult, A.add)
     ts(["md"], ["mki"], T.mki[:], T.md[:, 0:96], 1000000.0, None, A.mult)
-    ts(["si", "rc"], ["mk2"], T.mk2[:], T.si[:, 0:288], T.rc[:, 0:1], 1000000.0, A.is_lt, A.mult)
     ts(["mk2"], ["mk2"], T.mk2[:], T.mk2[:], -1.0, None, A.add)
     cp(T.ab0[:], T.ab0i[:], ["ab0i"], ["ab0"])
     cp(T.oa0[:], T.ab0i[:], ["ab0i"], ["oa0"])
+    for b in B4:
+        quant("eq", 128 * b, 128 * b + 128, "eb", 3 - b, ["eb"], ["eq%d" % b])
     dma("s", "dw", T.wq[:].bitcast(dt.uint8), T.wc[:], [], ["wq"])
     dma("s", "dw", T.wqs[:], T.ws[:], [], ["wq"])
     dma("s", "dv", T.vt[:], T.v[:], [], ["vt"])
@@ -192,46 +192,47 @@ def rank_program(g, core, T, topo):
         for k in range(8):
             z, zp = "_%d" % (k % 2), "_%d" % (1 - k % 2)
             if k == 0:
-                src, o, ak, oa, oak, lk, la, lb = T.ab0, [0, 3, 1], "ab0", T.oa0, "oa0", T.lk0, "lk0a", "lk0b"
+                src, o, ak, oa, oak, lk, lkk = T.ab0, [0, 3, 1], "ab0", T.oa0, "oa0", T.lk0, ["lk0a", "lk0b"]
             else:
-                src, o, ak, oa, oak, lk, la, lb = T["xs" + zp], [15, 63, 16], "xs" + zp, T["oa" + z], "oa" + z, T["lk" + zp], "lka" + zp, "lkb" + zp
+                src, o, ak, oa, oak, lk, lkk = T["xs" + zp], [15, 63, 16], "xs" + zp, T["oa" + z], "oa" + z, T["lk" + zp], ["lk%s%d" % (zp, i) for i in range(6)]
                 cp(oa[:], src[:, 15:96:16], [ak], [oak])
             a, b = src[:, o[0]:o[0] + 2 * o[2] + 1:o[2]], src[:, o[1]:o[1] + 2 * o[2] + 1:o[2]]
-            gs, cm, cs, dd, bb, m2, ln, lu, xg = [T[n + z] for n in "gs cm cs dd bb mm lk lu xg".split()]
+            gs, cm, cs, dd, ln, lu, xg = [T[n + z] for n in "gs cm cs dd lk lu xg".split()]
             tt(gs[:], T.sw[:, 384 * k:384 * k + 384].indirect(oa[:, 0:6]), T.mk1[:], A.min, [oak, "sw%da" % k, "sw%db" % k, "mk1a", "mk1b"], ["gs" + z])
             if k < 7:
-                ts([ak], ["bb" + z], bb[:], b, 384.0, None, A.add)
-                tt(dd[:, 0:3], a, lk[:, 0:3], A.subtract, [ak, la], ["da" + z])
-            tt(dd[:, 6:9], a, b, A.subtract, [ak], ["dc" + z])
-            if k < 7:
-                tt(dd[:, 3:6], lk[:, 3:6], bb[:], A.subtract, ["bb" + z, lb], ["db" + z])
+                tt(dd[:, 0:3], a, lk[:, 0:3], A.subtract, [ak] + lkk, ["da" + z])
+                tt(dd[:, 3:6], lk[:, 3:6], b, A.subtract, [ak] + lkk, ["db" + z])
             tt(cm[:], gs[:, 0:48], gs[:, 48:96], A.is_le, ["gs" + z], ["cm" + z])
-            scan(cs[:], cm[:], 48, ["cm" + z], ["cs" + z])
-            c = cs[:, 15:48:16]
             if k < 7:
-                tt(m2[:, 0:3], c, dd[:, 0:3], A.mult, ["cs" + z, "da" + z], ["ma" + z])
-                tt(m2[:, 3:6], c, dd[:, 3:6], A.mult, ["cs" + z, "db" + z], ["mb" + z])
-                tt(ln[:, 0:3], m2[:, 0:3], lk[:, 0:3], A.add, ["ma" + z, la], ["lka" + z])
-                tt(ln[:, 3:6], m2[:, 3:6], bb[:], A.add, ["mb" + z, "bb" + z], ["lkb" + z])
-                cp(lu[:], ln[:], ["lka" + z, "lkb" + z], ["lu" + z])
-                tt(xg[:], T.tb[:, 768 * k + 768:768 * k + 1536].indirect(lu[:, 0:6]), T.mki[:], A.min, ["lu" + z, "tb%d" % (k + 1), "mki"], ["xg" + z])
+                ts([ak], ["bb" + z], dd[:, 9:12], b, 384.0, None, A.add)
+            tt(dd[:, 6:9], a, b, A.subtract, [ak], ["dc" + z])
+            scan(cs[:], cm[:], 48, ["cm" + z], ["cs" + z])
+            for q in range(3):
+                cq, aq, bq = cs[:, 16 * q + 15:16 * q + 16], lk[:, q:q + 1], src[:, o[1] + o[2] * q:o[1] + o[2] * q + 1]
+                if k < 7:
+                    ts(["cs" + z, "da" + z] + lkk, ["lu%s%d" % (z, q)], lu[:, q:q + 1], cq, dd[:, q:q + 1], aq, A.mult, A.add)
+                    ts(["cs" + z, "db" + z, "bb" + z], ["lu%s%d" % (z, 3 + q)], lu[:, 3 + q:4 + q], cq, dd[:, 3 + q:4 + q], dd[:, 9 + q:10 + q], A.mult, A.add)
+                else:
+                    ts(["cs" + z, "dc" + z, ak], ["n87_%d" % q], T.n8[:, 21 + q:22 + q], cq, dd[:, 6 + q:7 + q], bq, A.mult, A.add)
+            if k < 7:
+                tt(xg[:], T.tb[:, 768 * k + 768:768 * k + 1536].indirect(lu[:, 0:6]), T.mki[:], A.min, ["lu%s%d" % (z, i) for i in range(6)] + ["tb%d" % (k + 1), "mki"], ["xg" + z])
                 scan(T["xs" + z][:], xg[:], 96, ["xg" + z], ["xs" + z])
-                for q in range(3):
-                    act(T.n8[:, 3 * k + q:3 * k + q + 1], cs[:, 16 * q + 15:16 * q + 16], F.Identity, ["cs" + z, "dc" + z, ak], ["n8%d_%d" % (k, q)],
-                        bias=src[:, o[1] + o[2] * q:o[1] + o[2] * q + 1], scale=dd[:, 6 + q:7 + q])
-            else:
-                tt(m2[:, 0:3], c, dd[:, 6:9], A.mult, ["cs" + z, "dc" + z], ["ma" + z])
-                tt(T.n8[:, 21:24], m2[:, 0:3], b, A.add, ["ma" + z, ak], ["n87_%d" % q for q in range(3)])
-            if k == 3:
-                for b2 in B4:
-                    act(T.vp[:, 384 * b2 + 288:384 * b2 + 384], bank(b2, 96, 32), F.Copy, ["pb%d" % b2], ["vp%db" % b2])
+                for q in range(9):
+                    i, m = q % 3, q // 3
+                    cq, bq = cs[:, 16 * i + 15:16 * i + 16], src[:, o[1] + o[2] * i:o[1] + o[2] * i + 1]
+                    act((T.n8[:, 3 * k + i:3 * k + i + 1] if m == 2 else ln[:, q:q + 1]), cq, F.Identity, ["cs" + z, "d" + "abc"[m] + z, ak] + lkk,
+                        ["n8%d_%d" % (k, i) if m == 2 else "lk%s%d" % (z, q)], bias=(bq if m else lk[:, i:i + 1]), scale=dd[:, q:q + 1])
+            if 1 <= k <= 4:
+                act(T.vp[:, 384 * k - 96:384 * k], bank(k - 1, 96, 32), F.Copy, ["pb%d" % (k - 1)], ["vp%db" % (k - 1)])
             if k == 0:
                 need("y", [], ["off"])
                 wr["off"], rd["off"] = [], []
             for h in range(6):
-                dma("y", "dn", T.off[16 * k:16 * k + 16, 3 * h:3 * h + 3], T.n8[16 * h:16 * h + 16, 3 * k:3 * k + 3], ["n8%d_%d" % (k, q) for q in range(3)], ["off"])
-        fill(T.inv[:], 288.0, ["inv"])
+                dma("s" if k == 7 and h > 2 else "y", "dn", T.off[16 * k:16 * k + 16, 3 * h:3 * h + 3], T.n8[16 * h:16 * h + 16, 3 * k:3 * k + 3], ["n8%d_%d" % (k, q) for q in range(3)], ["off"])
+        fill(T.inv0[:], 288.0, ["inv0"])
+        fill(T.inv1[:], 288.0, ["inv1"])
         cp(T.nu[:], T.off[:], ["off"], ["nu"])
+        cp(T.nx[:, 0:288:16], T.off[:], ["off"], ["nx"])
         for b in B4:
             w, rds = T.vp[:, 384 * b:384 * b + 384].indirect(T.nu[:, 0:18]), ["nu", "vp%da" % b, "vp%db" % b]
             if b < 2:
@@ -244,9 +245,8 @@ def rank_program(g, core, T, topo):
             act(T.tt[:, b:1152:4], bank(b), F.Copy, ["pb%d" % b], ["tt%d" % b], scale=0.03125)
         for b in B4:
             mm(4 + b, C, "eq", 128 * b, "qx", 96, ["eq%d" % b, "qa", "qb"])
-        tt(T.nf[:], T.idt[:, 0:400].indirect(T.nu[:, 0:18]), T.mk2[:], A.min, ["idt", "nu", "mk2"], ["nf"])
-        cp(T.nx[:, 0:288:16], T.off[:], ["off"], ["nx"])
         scan(T.ny[:], T.nx[:], 288, ["nx"], ["ny"])
+        tt(T.nf[:], T.idt[:, 0:400].indirect(T.nu[:, 0:18]), T.mk2[:], A.min, ["idt", "nu", "mk2"], ["nf"])
         tt(T.ne[:], T.nf[:], T.ny[:], A.is_equal, ["nf", "ny"], ["ne"])
         scan(T.nz[:], T.ne[:], 288, ["ne"], ["nz"])
         ts(["nz", "rd"], ["dm"], T.dm[:], T.nz[:, 15:288:16], 0.0, T.rd[:, 0:1], A.is_gt, A.mult)
@@ -257,9 +257,11 @@ def rank_program(g, core, T, topo):
             mm(b, C, "eq", 128 * b, "tq", 0, ["eq%d" % b, "tq"])
             act(T.dp[:, 304 * b:304 * b + 288], bank(b), F.Copy, ["pb%d" % b], ["dp%d" % b])
         for q in range(17, -1, -1):
-            cp(T.inv[:, 0:400].indirect(T.du[:, 2 * q:2 * q + 1]), T.idt[:, 16 * q:16 * q + 16], ["du", "idt"], ["inv"])
+            n = "inv%d" % (q % 2)
+            cp(T[n][:, 0:400].indirect(T.du[:, 2 * q:2 * q + 1]), T.idt[:, 16 * q:16 * q + 16], ["du", "idt"], [n])
         for n, i, j in (("b", 288, 384), ("o", 0, 288)):
-            tt(T.inm[:, i:j], T.inv[:, i:j], T.md[:, i:j], A.mult, ["inv", "md"], ["inm" + n])
+            tt(T.inn[:, i:j], T.inv0[:, i:j], T.inv1[:, i:j], A.min, ["inv0", "inv1"], ["inn" + n])
+            tt(T.inm[:, i:j], T.inn[:, i:j], T.md[:, i:j], A.mult, ["inn" + n, "md"], ["inm" + n])
             scan(T.ins[:, i:j], T.inm[:, i:j], j - i, ["inm" + n], ["ins" + n])
             cp(T.iu[:, i // 16:j // 16], T.ins[:, i + 15:j:16], ["ins" + n], ["iu" + n])
             if n == "b":

@@ -2,20 +2,22 @@ from concourse.mybir import dt, AluOpType as A, ActivationFunctionType as F
 
 C, H, E, R, N = 288, 96, 384, 3, 8
 BIG = 1e29
+HALVES = (("A", 0, 2), ("B", 2, 1))
 SCRATCH = {"pp": ("psum", [128, 4096], "float32")}
 for names, w in (("qx", 480), ("uq", 128), ("ur", 1024), ("vq", 128), ("wq", 512), ("eq", 512), ("mq", 288), ("tq", 288), ("bq", 128)):
     SCRATCH[names] = ("sbuf", [128, w], "float8_e4m3fn_x4")
     SCRATCH[names + "s"] = ("sbuf", [128, w], "uint8")
-for names, w, d in (("x0 xt mt tt uo", 1152, "bfloat16"), ("ut vt ub", 512, "bfloat16"), ("eb", 528, "bfloat16"), ("vp", 1536, "bfloat16"), ("dp", 1216, "bfloat16"),
-                    ("si md rst inn inm ins xf", 384, "float32"), ("idt inv0 inv1", 400, "float32"), ("mk1 mki", 96, "float32"),
+for names, w, d in [("x0 xt mt tt uo", 1152, "bfloat16"), ("ut vt ub", 512, "bfloat16"), ("eb", 528, "bfloat16"), ("vp", 1536, "bfloat16"), ("dp", 1216, "bfloat16"),
+                    ("si md rst inn inp inm ins xf", 384, "float32"), ("idt inv0 inv1 inv2", 400, "float32"), ("mk1 mki", 96, "float32"),
                     ("mk2 nf nx ny ne nz no yo", 288, "float32"), ("rc rd r2", 4, "float32"), ("lk0 ab0", 6, "float32"), ("lrf", 768, "float32"),
                     ("tb", 6144, "float32"), ("sw", 3072, "float32"), ("n8", 24, "float32"), ("off dm dn", 18, "float32"),
-                    ("gs_0 gs_1 xg_0 xg_1 xs_0 xs_1", 96, "float32"), ("cm_0 cm_1 cs_0 cs_1", 48, "float32"), ("dd_0 dd_1", 12, "float32"),
-                    ("lk_0 lk_1", 6, "float32"),
                     ("pi ri", 4, "int32"), ("ji", 3, "int32"), ("uli", 64, "int32"), ("lri", 48, "int32"), ("ab0i", 6, "int32"),
-                    ("ul", 64, "uint16"), ("lru", 48, "uint16"), ("oa0 oa_0 oa_1 lu_0 lu_1", 6, "uint16"), ("nu", 18, "uint16"), ("du", 36, "uint16"), ("iu", 24, "uint16")):
+                    ("ul", 64, "uint16"), ("lru", 48, "uint16"), ("nu", 18, "uint16"), ("du", 36, "uint16"), ("iu", 24, "uint16")] + [
+                    (" ".join(n + f + p for n in ns.split() for p in "01"), m * nb, d) for f, q0, nb in HALVES for ns, m, d in
+                    (("gs xg xs", 32, "float32"), ("cm cs", 16, "float32"), ("dd", 4, "float32"), ("lk", 2, "float32"), ("oa lu", 2, "uint16"))]:
     for name in names.split():
         SCRATCH[name] = ("sbuf", [128, w], d)
+SCRATCH["ozA"], SCRATCH["ozB"] = ("sbuf", [128, 4], "uint16"), ("sbuf", [128, 2], "uint16")
 SEMAPHORES = "sv st sa sg dx dx2 dl da du dw dv dn brd bl ret rl do dp".split() + ["dt%d" % k for k in range(8)]
 B4 = range(4)
 
@@ -124,10 +126,10 @@ def rank_program(g, core, T, topo):
         arrive("brd", nxt, "qr")
 
     dma("y", "dx", T.x0[:, 0:512], T.x[:, 0:512], [], ["x0a"])
+    dma("s", "du", T.ut[:], T.u[:], [], ["ut"])
+    dma("y", "dx2", T.x0[:, 512:1152], T.x[:, 512:1152], [], ["x0b"])
     dma("s", "dl", T.lri[:, 0:24], T.lf[:], [], ["lri"])
     dma("s", "dl", T.lri[:, 24:48], T.rt[:], [], ["lri"])
-    dma("y", "dx2", T.x0[:, 512:1152], T.x[:, 512:1152], [], ["x0b"])
-    dma("s", "du", T.ut[:], T.u[:], [], ["ut"])
     for h in range(8):
         c = 3 * h if h < 6 else 0
         dma("y", "da", T.ab0i[16 * h:16 * h + 16, 0:3], T.lf[0:16, c:c + 3], [], ["ab0i"])
@@ -148,21 +150,21 @@ def rank_program(g, core, T, topo):
     cp(T.rc[:], T.ri[:], ["ri"], ["rc"])
     ts(["rc"], ["rd"], T.rd[:], T.rc[:], 384.0, None, A.add)
     ts(["rc"], ["r2"], T.r2[:], T.rc[:], -2.0, None, A.mult)
-    ts(["ji", "r2"], ["lk0a"], T.lk0[:, 0:3], T.ji[:], T.r2[:, 0:1], None, A.add)
-    ts(["ji", "r2"], ["lk0b"], T.lk0[:, 3:6], T.ji[:], T.r2[:, 0:1], None, A.add)
+    for i in range(2):
+        ts(["ji", "r2"], ["lk0%d" % i], T.lk0[:, 3 * i:3 * i + 3], T.ji[:], T.r2[:, 0:1], None, A.add)
     quant("qx", 96, 224, "x0", 0, ["x0a"], ["qa"])
     send_border()
     op("g", g.affine_select, ["eb"], ["eb"], T.eb[:], T.eb[:], [[1, 528]], A.is_equal, 0.0, -3, -4)
-    cp(T.lru[:], T.lri[:], ["lri"], ["lru"])
-    cp(T.lrf[:, 0:384], T.idt[:, 0:400].indirect(T.lru[:, 0:24]), ["lru", "idt"], ["lrfa"])
-    act(T.lrf[:, 384:768], T.idt[:, 0:400].indirect(T.lru[:, 24:48]), F.Copy, ["lru", "idt"], ["lrfb"])
-    for k in range(1, 8):
-        for h in range(8):
-            dma("y", "dt%d" % k, T.tb[16 * h:16 * h + 16, 768 * k:768 * k + 768], T.lrf[16 * k:16 * k + 16, :], ["lrfa", "lrfb"], ["tb%d" % k])
     quant("uq", 0, 128, "ut", 0, ["ut"], ["uq"])
     cp(T.ur[:, 0:1024].bitcast(dt.uint32), T.uq[:, 0:128].bitcast(dt.uint32).indirect(T.ul[:, 0:64]), ["uq", "ul"], ["ur"])
     act(T.urs[:, 0:1024], T.uqs[:, 0:128].indirect(T.ul[:, 0:64]), F.Copy, ["uq", "ul"], ["urs"])
     quant("qx", 224, 384, "x0", 512, ["x0b"], ["qb"])
+    cp(T.lru[:], T.lri[:], ["lri"], ["lru"])
+    cp(T.lrf[:, 0:384], T.idt[:, 0:400].indirect(T.lru[:, 0:24]), ["lru", "idt"], ["lrfa"])
+    cp(T.lrf[:, 384:768], T.idt[:, 0:400].indirect(T.lru[:, 24:48]), ["lru", "idt"], ["lrfb"])
+    for k in range(1, 8):
+        for h in range(8):
+            dma("y", "dt%d" % k, T.tb[16 * h:16 * h + 16, 768 * k:768 * k + 768], T.lrf[16 * k:16 * k + 16, :], ["lrfa", "lrfb"], ["tb%d" % k])
     ts(["si", "rc"], ["md"], T.md[:], T.si[:], T.rc[:, 0:1], None, A.is_equal)
     ts(["si"], ["rst"], T.rst[:], T.si[:], 0.0, None, A.is_gt)
     ts(["si", "rc"], ["mk2"], T.mk2[:], T.si[:, 0:288], T.rc[:, 0:1], 1000000.0, A.is_lt, A.mult)
@@ -170,12 +172,69 @@ def rank_program(g, core, T, topo):
     ts(["md"], ["mki"], T.mki[:], T.md[:, 0:96], 1000000.0, None, A.mult)
     ts(["mk2"], ["mk2"], T.mk2[:], T.mk2[:], -1.0, None, A.add)
     cp(T.ab0[:], T.ab0i[:], ["ab0i"], ["ab0"])
-    cp(T.oa0[:], T.ab0i[:], ["ab0i"], ["oa0"])
+    for f, q0, nb in HALVES:
+        for i in range(2):
+            cp(T["oz" + f][:, i * nb:i * nb + nb], T.ab0i[:, 3 * i + q0:3 * i + q0 + nb], ["ab0i"], ["oz%s%d" % (f, i)])
     for b in B4:
         quant("eq", 128 * b, 128 * b + 128, "eb", 3 - b, ["eb"], ["eq%d" % b])
     dma("s", "dw", T.wq[:].bitcast(dt.uint8), T.wc[:], [], ["wq"])
     dma("s", "dw", T.wqs[:], T.ws[:], [], ["wq"])
     dma("s", "dv", T.vt[:], T.v[:], [], ["vt"])
+
+    def step(k):
+        c = {}
+        for f, q0, nb in HALVES:
+            z, zp = f + str(k % 2), f + str(1 - k % 2)
+            gs, xg, xs, cm, cs, dd, ln, oa, lu = [T[n + z] for n in "gs xg xs cm cs dd lk oa lu".split()]
+            w, ws = 16 * nb, 384 * k
+            if k == 0:
+                src, ak, oa, oak, st = T.ab0, "ab0", T["oz" + f], ["oz%s%d" % (f, i) for i in range(2)], 1
+                ac, bc, lkk = [q0 + i for i in range(nb)], [3 + q0 + i for i in range(nb)], ["lk00", "lk01"]
+                l, kk = T.lk0[:, q0:q0 + nb], T.lk0[:, 3 + q0:3 + q0 + nb]
+            else:
+                src, ak, oak, st = T["xs" + zp], "xs" + zp, ["oa" + z], 16
+                ac, bc = [15 + 16 * i for i in range(nb)], [15 + 16 * (nb + i) for i in range(nb)]
+                l, kk, lkk = T["lk" + zp][:, 0:nb], T["lk" + zp][:, nb:2 * nb], ["lk%s_%d" % (zp, i) for i in range(2 * nb)]
+                c["oa" + f] = lambda oa=oa, x=src[:, 15:2 * w:16], r=ak, o=oak: cp(oa[:], x, [r], o)
+            a, b = src[:, ac[0]:ac[-1] + 1:st], src[:, bc[0]:bc[-1] + 1:st]
+
+            def d(i, nb=nb, dd=dd):
+                return dd[:, i * nb:i * nb + nb]
+            c["sg" + f] = lambda gs=gs, w=w, oa=oa, nb=nb, o=oak, z=z: tt(gs[:], T.sw[:, ws:ws + 384].indirect(oa[:, 0:2 * nb]), T.mk1[:, 48 - w:48 + w], A.min, o + ["sw%da" % k, "sw%db" % k, "mk1a", "mk1b"], ["gs" + z])
+            c["da" + f] = lambda d=d, a=a, l=l, r=[ak] + lkk, z=z: tt(d(0), a, l, A.subtract, r, ["da" + z])
+            c["db" + f] = lambda d=d, b=b, kk=kk, r=[ak] + lkk, z=z: tt(d(1), kk, b, A.subtract, r, ["db" + z])
+            c["dc" + f] = lambda d=d, a=a, b=b, r=[ak], z=z: tt(d(2), a, b, A.subtract, r, ["dc" + z])
+            c["bb" + f] = lambda d=d, b=b, r=[ak], z=z: ts(r, ["bb" + z], d(3), b, 384.0, None, A.add)
+            c["cm" + f] = lambda cm=cm, gs=gs, w=w, z=z: tt(cm[:], gs[:, 0:w], gs[:, w:2 * w], A.is_le, ["gs" + z], ["cm" + z])
+            c["sc" + f] = lambda cs=cs, cm=cm, w=w, z=z: scan(cs[:], cm[:], w, ["cm" + z], ["cs" + z])
+
+            def sel(cs=cs, dd=dd, nb=nb, lu=lu, z=z, src=src, bc=bc, lkk=lkk, q0=q0, ak=ak, zp=zp):
+                for i in range(nb):
+                    cq = cs[:, 16 * i + 15:16 * i + 16]
+                    lq = T.lk0[:, q0 + i:q0 + i + 1] if k == 0 else T["lk" + zp][:, i:i + 1]
+                    if k < 7:
+                        ts(["cs" + z, "da" + z] + lkk, ["lu%s_%d" % (z, i)], lu[:, i:i + 1], cq, dd[:, i:i + 1], lq, A.mult, A.add)
+                        ts(["cs" + z, "db" + z, "bb" + z], ["lu%s_%d" % (z, nb + i)], lu[:, nb + i:nb + i + 1], cq, dd[:, nb + i:nb + i + 1], dd[:, 3 * nb + i:3 * nb + i + 1], A.mult, A.add)
+                    else:
+                        ts(["cs" + z, "dc" + z, ak], ["n87_%d" % (q0 + i)], T.n8[:, 21 + q0 + i:22 + q0 + i], cq, dd[:, 2 * nb + i:2 * nb + i + 1], src[:, bc[i]:bc[i] + 1], A.mult, A.add)
+            c["se" + f] = sel
+            c["xg" + f] = lambda xg=xg, lu=lu, w=w, nb=nb, z=z: tt(xg[:], T.tb[:, 2 * ws + 768:2 * ws + 1536].indirect(lu[:, 0:2 * nb]), T.mki[:, 0:2 * w], A.min, ["lu%s_%d" % (z, i) for i in range(2 * nb)] + ["tb%d" % (k + 1), "mki"], ["xg" + z])
+            c["xs" + f] = lambda xs=xs, xg=xg, w=w, z=z: scan(xs[:], xg[:], 2 * w, ["xg" + z], ["xs" + z])
+
+            def ends(m, cs=cs, dd=dd, nb=nb, ln=ln, z=z, src=src, bc=bc, lkk=lkk, q0=q0, ak=ak, zp=zp):
+                for i in range(nb):
+                    lq = T.lk0[:, q0 + i:q0 + i + 1] if k == 0 else T["lk" + zp][:, i:i + 1]
+                    out, key = (T.n8[:, 3 * k + q0 + i:3 * k + q0 + i + 1], "n8%d_%d" % (k, q0 + i)) if m == 2 else (ln[:, nb * m + i:nb * m + i + 1], "lk%s_%d" % (z, nb * m + i))
+                    act(out, cs[:, 16 * i + 15:16 * i + 16], F.Identity, ["cs" + z, "d" + "abc"[m] + z, ak] + lkk, [key],
+                        bias=src[:, bc[i]:bc[i] + 1] if m else lq, scale=dd[:, m * nb + i:m * nb + i + 1])
+            c["en" + f] = ends
+        order = "sgA sgB daA dbA cmA cmB bbA dcA scA scB daB dbB bbB seA seB dcB xgA xgB xsA xsB" if k < 7 else "sgA sgB dcA dcB cmA cmB scA scB seA seB"
+        for n in (("oaA oaB " if k else "") + order).split():
+            c[n]()
+        if k < 7:
+            for m in range(3):
+                for f, q0, nb in HALVES:
+                    c["en" + f](m)
 
     for t in range(R):
         for k in range(8):
@@ -190,38 +249,7 @@ def rank_program(g, core, T, topo):
         for b in B4:
             mm(b, 128, "eq", 128 * b, "qx", 352, ["eq%d" % b, "qb", "qr"])
         for k in range(8):
-            z, zp = "_%d" % (k % 2), "_%d" % (1 - k % 2)
-            if k == 0:
-                src, o, ak, oa, oak, lk, lkk = T.ab0, [0, 3, 1], "ab0", T.oa0, "oa0", T.lk0, ["lk0a", "lk0b"]
-            else:
-                src, o, ak, oa, oak, lk, lkk = T["xs" + zp], [15, 63, 16], "xs" + zp, T["oa" + z], "oa" + z, T["lk" + zp], ["lk%s%d" % (zp, i) for i in range(6)]
-                cp(oa[:], src[:, 15:96:16], [ak], [oak])
-            a, b = src[:, o[0]:o[0] + 2 * o[2] + 1:o[2]], src[:, o[1]:o[1] + 2 * o[2] + 1:o[2]]
-            gs, cm, cs, dd, ln, lu, xg = [T[n + z] for n in "gs cm cs dd lk lu xg".split()]
-            tt(gs[:], T.sw[:, 384 * k:384 * k + 384].indirect(oa[:, 0:6]), T.mk1[:], A.min, [oak, "sw%da" % k, "sw%db" % k, "mk1a", "mk1b"], ["gs" + z])
-            if k < 7:
-                tt(dd[:, 0:3], a, lk[:, 0:3], A.subtract, [ak] + lkk, ["da" + z])
-                tt(dd[:, 3:6], lk[:, 3:6], b, A.subtract, [ak] + lkk, ["db" + z])
-            tt(cm[:], gs[:, 0:48], gs[:, 48:96], A.is_le, ["gs" + z], ["cm" + z])
-            if k < 7:
-                ts([ak], ["bb" + z], dd[:, 9:12], b, 384.0, None, A.add)
-            tt(dd[:, 6:9], a, b, A.subtract, [ak], ["dc" + z])
-            scan(cs[:], cm[:], 48, ["cm" + z], ["cs" + z])
-            for q in range(3):
-                cq, aq, bq = cs[:, 16 * q + 15:16 * q + 16], lk[:, q:q + 1], src[:, o[1] + o[2] * q:o[1] + o[2] * q + 1]
-                if k < 7:
-                    ts(["cs" + z, "da" + z] + lkk, ["lu%s%d" % (z, q)], lu[:, q:q + 1], cq, dd[:, q:q + 1], aq, A.mult, A.add)
-                    ts(["cs" + z, "db" + z, "bb" + z], ["lu%s%d" % (z, 3 + q)], lu[:, 3 + q:4 + q], cq, dd[:, 3 + q:4 + q], dd[:, 9 + q:10 + q], A.mult, A.add)
-                else:
-                    ts(["cs" + z, "dc" + z, ak], ["n87_%d" % q], T.n8[:, 21 + q:22 + q], cq, dd[:, 6 + q:7 + q], bq, A.mult, A.add)
-            if k < 7:
-                tt(xg[:], T.tb[:, 768 * k + 768:768 * k + 1536].indirect(lu[:, 0:6]), T.mki[:], A.min, ["lu%s%d" % (z, i) for i in range(6)] + ["tb%d" % (k + 1), "mki"], ["xg" + z])
-                scan(T["xs" + z][:], xg[:], 96, ["xg" + z], ["xs" + z])
-                for q in range(9):
-                    i, m = q % 3, q // 3
-                    cq, bq = cs[:, 16 * i + 15:16 * i + 16], src[:, o[1] + o[2] * i:o[1] + o[2] * i + 1]
-                    act((T.n8[:, 3 * k + i:3 * k + i + 1] if m == 2 else ln[:, q:q + 1]), cq, F.Identity, ["cs" + z, "d" + "abc"[m] + z, ak] + lkk,
-                        ["n8%d_%d" % (k, i) if m == 2 else "lk%s%d" % (z, q)], bias=(bq if m else lk[:, i:i + 1]), scale=dd[:, q:q + 1])
+            step(k)
             if 1 <= k <= 4:
                 act(T.vp[:, 384 * k - 96:384 * k], bank(k - 1, 96, 32), F.Copy, ["pb%d" % (k - 1)], ["vp%db" % (k - 1)])
             if k == 0:
@@ -229,8 +257,8 @@ def rank_program(g, core, T, topo):
                 wr["off"], rd["off"] = [], []
             for h in range(6):
                 dma("s" if k == 7 and h > 2 else "y", "dn", T.off[16 * k:16 * k + 16, 3 * h:3 * h + 3], T.n8[16 * h:16 * h + 16, 3 * k:3 * k + 3], ["n8%d_%d" % (k, q) for q in range(3)], ["off"])
-        fill(T.inv0[:], 288.0, ["inv0"])
-        fill(T.inv1[:], 288.0, ["inv1"])
+        for i in range(3):
+            fill(T["inv%d" % i][:], 288.0, ["inv%d" % i])
         cp(T.nu[:], T.off[:], ["off"], ["nu"])
         cp(T.nx[:, 0:288:16], T.off[:], ["off"], ["nx"])
         for b in B4:
@@ -239,41 +267,53 @@ def rank_program(g, core, T, topo):
                 act(T.mt[:, b:1152:4], w, F.Copy, rds, ["mt%d" % b])
             else:
                 cp(T.mt[:, b:1152:4], w, rds, ["mt%d" % b])
+            if b == 2:
+                scan(T.ny[:], T.nx[:], 288, ["nx"], ["ny"])
         quant("mq", 0, 288, "mt", 0, each("mt%d"), ["mq"])
         for b in B4:
             mm(b, C, "wq", 128 * b, "mq", 0, ["wq", "mq"])
             act(T.tt[:, b:1152:4], bank(b), F.Copy, ["pb%d" % b], ["tt%d" % b], scale=0.03125)
         for b in B4:
             mm(4 + b, C, "eq", 128 * b, "qx", 96, ["eq%d" % b, "qa", "qb"])
-        scan(T.ny[:], T.nx[:], 288, ["nx"], ["ny"])
         tt(T.nf[:], T.idt[:, 0:400].indirect(T.nu[:, 0:18]), T.mk2[:], A.min, ["idt", "nu", "mk2"], ["nf"])
         tt(T.ne[:], T.nf[:], T.ny[:], A.is_equal, ["nf", "ny"], ["ne"])
         scan(T.nz[:], T.ne[:], 288, ["ne"], ["nz"])
         ts(["nz", "rd"], ["dm"], T.dm[:], T.nz[:, 15:288:16], 0.0, T.rd[:, 0:1], A.is_gt, A.mult)
         tt(T.dn[:], T.dm[:], T.off[:], A.max, ["dm", "off"], ["dn"])
-        cp(T.du[:, 0:36:2], T.dn[:], ["dn"], ["du"])
         quant("tq", 0, 288, "tt", 0, each("tt%d"), ["tq"])
+        cp(T.du[:, 0:36:2], T.dn[:], ["dn"], ["du"])
         for b in B4:
             mm(b, C, "eq", 128 * b, "tq", 0, ["eq%d" % b, "tq"])
             act(T.dp[:, 304 * b:304 * b + 288], bank(b), F.Copy, ["pb%d" % b], ["dp%d" % b])
         for q in range(17, -1, -1):
-            n = "inv%d" % (q % 2)
+            n = "inv%d" % (q % 3)
             cp(T[n][:, 0:400].indirect(T.du[:, 2 * q:2 * q + 1]), T.idt[:, 16 * q:16 * q + 16], ["du", "idt"], [n])
-        for n, i, j in (("b", 288, 384), ("o", 0, 288)):
-            tt(T.inn[:, i:j], T.inv0[:, i:j], T.inv1[:, i:j], A.min, ["inv0", "inv1"], ["inn" + n])
-            tt(T.inm[:, i:j], T.inn[:, i:j], T.md[:, i:j], A.mult, ["inn" + n, "md"], ["inm" + n])
-            scan(T.ins[:, i:j], T.inm[:, i:j], j - i, ["inm" + n], ["ins" + n])
-            cp(T.iu[:, i // 16:j // 16], T.ins[:, i + 15:j:16], ["ins" + n], ["iu" + n])
-            if n == "b":
-                for b in B4:
-                    w, rds = T.dp[:, 304 * b:304 * b + 304].indirect(T.iu[:, 18:24]), ["iub", "dp%d" % b, "dpz%d" % b]
-                    if b < 2:
-                        act(T.ub[:, b:384:4], w, F.Copy, rds, ["ub%d" % b])
-                    else:
-                        cp(T.ub[:, b:384:4], w, rds, ["ub%d" % b])
-                quant("bq", 0, 128, "ub", 0, each("ub%d") + ["ubz"], ["bq"])
-                send(nxt, "ret", "rl", "qx", 0, "bq", 0, ["bq"])
-                arrive("ret", prv, "qt")
+
+        def ext(n, i):
+            a, b = (288, 384) if n == "b" else (0, 288)
+            if i == 0:
+                tt(T.inn[:, a:b], T.inv0[:, a:b], T.inv1[:, a:b], A.min, ["inv0", "inv1"], ["inn" + n])
+            elif i == 1:
+                tt(T.inp[:, a:b], T.inn[:, a:b], T.inv2[:, a:b], A.min, ["inn" + n, "inv2"], ["inp" + n])
+            elif i == 2:
+                tt(T.inm[:, a:b], T.inp[:, a:b], T.md[:, a:b], A.mult, ["inp" + n, "md"], ["inm" + n])
+            elif i == 3:
+                scan(T.ins[:, a:b], T.inm[:, a:b], b - a, ["inm" + n], ["ins" + n])
+            else:
+                cp(T.iu[:, a // 16:b // 16], T.ins[:, a + 15:b:16], ["ins" + n], ["iu" + n])
+        for s in "b0 o0 b1 b2 b3 b4 o1".split():
+            ext(s[0], int(s[1]))
+        for b in B4:
+            w, rds = T.dp[:, 304 * b:304 * b + 304].indirect(T.iu[:, 18:24]), ["iub", "dp%d" % b, "dpz%d" % b]
+            if b < 2:
+                act(T.ub[:, b:384:4], w, F.Copy, rds, ["ub%d" % b])
+            else:
+                cp(T.ub[:, b:384:4], w, rds, ["ub%d" % b])
+        quant("bq", 0, 128, "ub", 0, each("ub%d") + ["ubz"], ["bq"])
+        send(nxt, "ret", "rl", "qx", 0, "bq", 0, ["bq"])
+        arrive("ret", prv, "qt")
+        for i in (2, 3, 4):
+            ext("o", i)
         for b in B4:
             w, rds, o = T.dp[:, 304 * b:304 * b + 304].indirect(T.iu[:, 0:18]), ["iuo", "dp%d" % b, "dpz%d" % b], T.uo[:, 288 * b:288 * b + 288]
             if b % 2 == 0:

from concourse.mybir import dt, AluOpType as A, ActivationFunctionType as F

C, H, E, R, N = 288, 96, 384, 3, 8
BIG = 1e29
HALVES = (("A", 0, 2), ("B", 2, 1))
SCRATCH = {"pp": ("psum", [128, 4096], "float32")}
for names, w in (("qx", 480), ("uq", 128), ("ur", 1024), ("vq", 128), ("wq", 512), ("eq", 512), ("mq", 288), ("tq", 288), ("bq", 128)):
    SCRATCH[names] = ("sbuf", [128, w], "float8_e4m3fn_x4")
    SCRATCH[names + "s"] = ("sbuf", [128, w], "uint8")
for names, w, d in [("x0 xt mt tt uo", 1152, "bfloat16"), ("ut vt ub", 512, "bfloat16"), ("eb", 528, "bfloat16"), ("vp", 1536, "bfloat16"), ("dp", 1216, "bfloat16"),
                    ("si md rst inn inp inm ins xf", 384, "float32"), ("idt inv0 inv1 inv2", 400, "float32"), ("mk1 mki", 96, "float32"),
                    ("mk2 nf nx ny ne nz no yo", 288, "float32"), ("rc rd r2", 4, "float32"), ("lk0 ab0", 6, "float32"), ("lrf", 768, "float32"),
                    ("tb", 6144, "float32"), ("sw", 3072, "float32"), ("n8", 24, "float32"), ("off dm dn", 18, "float32"),
                    ("pi ri", 4, "int32"), ("ji", 3, "int32"), ("uli", 64, "int32"), ("lri", 48, "int32"), ("ab0i", 6, "int32"),
                    ("ul", 64, "uint16"), ("lru", 48, "uint16"), ("nu", 18, "uint16"), ("du", 36, "uint16"), ("iu", 24, "uint16")] + [
                    (" ".join(n + f + p for n in ns.split() for p in "01"), m * nb, d) for f, q0, nb in HALVES for ns, m, d in
                    (("gs xg xs", 32, "float32"), ("cm cs", 16, "float32"), ("dd", 4, "float32"), ("lk", 2, "float32"), ("oa lu", 2, "uint16"))]:
    for name in names.split():
        SCRATCH[name] = ("sbuf", [128, w], d)
SCRATCH["ozA"], SCRATCH["ozB"] = ("sbuf", [128, 4], "uint16"), ("sbuf", [128, 2], "uint16")
SEMAPHORES = "sv st sa sg dx dx2 dl da du dw dv dn brd bl ret rl do dp".split() + ["dt%d" % k for k in range(8)]
B4 = range(4)


def rank_program(g, core, T, topo):
    rank = T.rank_of(core)
    if rank is None:
        return
    nxt, prv = T.cores[(rank + 1) % N], T.cores[(rank - 1) % N]
    V, P, S = g.vector, g.tensor, g.scalar
    eng = {"v": V, "t": P, "s": S, "g": g, "y": g.sync}
    own = {"v": "sv", "t": "st", "s": "sa", "g": "sg"}
    total = {n: 0 for n in SEMAPHORES}
    know = {q: {} for q in eng}
    snaps = {n: [] for n in SEMAPHORES}
    wr, rd = {}, {}

    def learn(q, sem, val):
        k = know[q]
        if k.get(sem, 0) >= val:
            return
        eng[q].wait_ge(T.sem[sem], val)
        k[sem] = val
        for v, s in snaps[sem]:
            if v <= val:
                for a, b in s.items():
                    k[a] = max(k.get(a, 0), b)

    def need(q, reads, writes):
        w = {}
        l = [r for key in list(reads) + list(writes) for r in wr.get(key, [])]
        l += [r for key in writes for r in rd.get(key, []) if r[3] or r[0] != q]
        for oq, sem, val, d in l:
            if know[q].get(sem, 0) < val:
                w[sem] = max(w.get(sem, 0), total[sem] if d else val)
        for sem in w:
            learn(q, sem, w[sem])

    def done(q, sem, inc, reads, writes, d, more=False):
        total[sem] += inc
        snaps[sem].append((total[sem], dict(know[q])))
        rec = (q, sem, total[sem], d)
        for key in writes:
            wr[key] = (wr.get(key, []) if more else []) + [rec]
            if not more:
                rd[key] = []
        for key in reads:
            rd.setdefault(key, []).append(rec)

    def op(q, f, reads, writes, *a, **kw):
        need(q, reads, writes)
        f(*a, **kw).then_inc(T.sem[own[q]], 1)
        done(q, own[q], 1, reads, writes, False)

    def dma(q, sem, out, in_, reads, writes, more=True):
        need(q, reads, [] if more else writes)
        eng[q].dma_start(out, in_).then_inc(T.sem[sem], 16)
        done(q, sem, 16, reads, writes, True, more)

    def send(dst, rsem, lsem, q, d0, s, s0, reads):
        need("g", reads, [])
        rid, pid = topo.addr(dst, core)
        for o, i in ((T[q][:, d0:d0 + H].bitcast(dt.uint8), T[s][:, s0:s0 + H].bitcast(dt.uint8)), (T[q + "s"][:, d0:d0 + H], T[s + "s"][:, s0:s0 + H])):
            g.remote_dma(o, i, T.sem[rsem], T.sem[lsem], pid, rid, topo.mask(core, dst))
            done("g", lsem, len(topo.engines(core, dst)), reads, [], True)

    def arrive(rsem, src, key):
        total[rsem] += 2 * len(topo.engines(src, core))
        wr[key], rd[key] = [("r", rsem, total[rsem], True)], []

    def bank(k, n=C, a=0):
        return T.pp[:, 512 * k + a:512 * k + a + n]

    def mm(k, n, l, l0, r, r0, reads):
        op("t", P.matmul_mx, reads, ["pb%d" % k], bank(k, n), T[l][:, l0:l0 + 128], T[l + "s"][:, l0:l0 + 128], T[r][:, r0:r0 + n], T[r + "s"][:, r0:r0 + n], True, True)

    def act(out, in_, func, reads, writes, **kw):
        op("s", S.activation, reads, writes, out, in_, func, **kw)

    def tt(out, a, b, o, reads, writes):
        op("v", V.tensor_tensor, reads, writes, out, a, b, o)

    def ts(reads, writes, *a):
        op("v", V.tensor_scalar, reads, writes, *a)

    def cp(out, a, reads, writes):
        op("v", V.tensor_copy, reads, writes, out, a)

    def fill(out, c, writes):
        op("v", V.memset, [], writes, out, c)

    def scan(out, d1, n, reads, writes):
        op("v", V.tensor_tensor_scan, ["rst"] + reads, writes, out, T.rst[:, 0:n], d1, 0.0, A.mult, A.add)

    def quant(q, a, b, tile, t0, reads, writes):
        op("v", V.quantize_mx, reads, writes, T[q][:, a:b], T[q + "s"][:, a:b], T[tile][:, t0:t0 + 4 * (b - a)])

    def iota(n, pattern, cm, **kw):
        op("g", g.iota, [], [n], T[n][:], pattern, 0, cm, **kw)

    def each(s):
        return [s % b for b in B4]

    def send_border():
        send(prv, "brd", "bl", "qx", 384, "qx", 96, ["qa"])
        arrive("brd", nxt, "qr")

    dma("y", "dx", T.x0[:, 0:512], T.x[:, 0:512], [], ["x0a"])
    dma("s", "du", T.ut[:], T.u[:], [], ["ut"])
    dma("y", "dx2", T.x0[:, 512:1152], T.x[:, 512:1152], [], ["x0b"])
    dma("s", "dl", T.lri[:, 0:24], T.lf[:], [], ["lri"])
    dma("s", "dl", T.lri[:, 24:48], T.rt[:], [], ["lri"])
    for h in range(8):
        c = 3 * h if h < 6 else 0
        dma("y", "da", T.ab0i[16 * h:16 * h + 16, 0:3], T.lf[0:16, c:c + 3], [], ["ab0i"])
        dma("y", "da", T.ab0i[16 * h:16 * h + 16, 3:6], T.rt[0:16, c:c + 3], [], ["ab0i"])
    iota("pi", [[0, 4]], 1)
    iota("uli", [[16, 8], [0, 8]], 0)
    iota("ji", [[16, 3]], 3)
    iota("si", [[0, 24], [1, 16]], 0, allow_small_or_imprecise_dtypes=True)
    iota("idt", [[1, 400]], 0, allow_small_or_imprecise_dtypes=True)
    fill(T.eb[:], 1.0, ["eb"])
    fill(T.ub[:, 384:512], 0.0, ["ubz"])
    for b in B4:
        fill(T.dp[:, 304 * b + 288:304 * b + 304], 0.0, ["dpz%d" % b])
    fill(T.mk1[:, 0:48], BIG, ["mk1a"])
    fill(T.nx[:], 0.0, ["nx"])
    cp(T.ul[:], T.uli[:], ["uli"], ["ul"])
    ts(["pi"], ["ri"], T.ri[:], T.pi[:], 15, None, A.bitwise_and)
    cp(T.rc[:], T.ri[:], ["ri"], ["rc"])
    ts(["rc"], ["rd"], T.rd[:], T.rc[:], 384.0, None, A.add)
    ts(["rc"], ["r2"], T.r2[:], T.rc[:], -2.0, None, A.mult)
    for i in range(2):
        ts(["ji", "r2"], ["lk0%d" % i], T.lk0[:, 3 * i:3 * i + 3], T.ji[:], T.r2[:, 0:1], None, A.add)
    quant("qx", 96, 224, "x0", 0, ["x0a"], ["qa"])
    send_border()
    op("g", g.affine_select, ["eb"], ["eb"], T.eb[:], T.eb[:], [[1, 528]], A.is_equal, 0.0, -3, -4)
    quant("uq", 0, 128, "ut", 0, ["ut"], ["uq"])
    cp(T.ur[:, 0:1024].bitcast(dt.uint32), T.uq[:, 0:128].bitcast(dt.uint32).indirect(T.ul[:, 0:64]), ["uq", "ul"], ["ur"])
    act(T.urs[:, 0:1024], T.uqs[:, 0:128].indirect(T.ul[:, 0:64]), F.Copy, ["uq", "ul"], ["urs"])
    quant("qx", 224, 384, "x0", 512, ["x0b"], ["qb"])
    cp(T.lru[:], T.lri[:], ["lri"], ["lru"])
    cp(T.lrf[:, 0:384], T.idt[:, 0:400].indirect(T.lru[:, 0:24]), ["lru", "idt"], ["lrfa"])
    cp(T.lrf[:, 384:768], T.idt[:, 0:400].indirect(T.lru[:, 24:48]), ["lru", "idt"], ["lrfb"])
    for k in range(1, 8):
        for h in range(8):
            dma("y", "dt%d" % k, T.tb[16 * h:16 * h + 16, 768 * k:768 * k + 768], T.lrf[16 * k:16 * k + 16, :], ["lrfa", "lrfb"], ["tb%d" % k])
    ts(["si", "rc"], ["md"], T.md[:], T.si[:], T.rc[:, 0:1], None, A.is_equal)
    ts(["si"], ["rst"], T.rst[:], T.si[:], 0.0, None, A.is_gt)
    ts(["si", "rc"], ["mk2"], T.mk2[:], T.si[:, 0:288], T.rc[:, 0:1], 1000000.0, A.is_lt, A.mult)
    ts(["md"], ["mk1b"], T.mk1[:, 48:96], T.md[:, 0:48], BIG, -1.0, A.mult, A.add)
    ts(["md"], ["mki"], T.mki[:], T.md[:, 0:96], 1000000.0, None, A.mult)
    ts(["mk2"], ["mk2"], T.mk2[:], T.mk2[:], -1.0, None, A.add)
    cp(T.ab0[:], T.ab0i[:], ["ab0i"], ["ab0"])
    for f, q0, nb in HALVES:
        for i in range(2):
            cp(T["oz" + f][:, i * nb:i * nb + nb], T.ab0i[:, 3 * i + q0:3 * i + q0 + nb], ["ab0i"], ["oz%s%d" % (f, i)])
    for b in B4:
        quant("eq", 128 * b, 128 * b + 128, "eb", 3 - b, ["eb"], ["eq%d" % b])
    dma("s", "dw", T.wq[:].bitcast(dt.uint8), T.wc[:], [], ["wq"])
    dma("s", "dw", T.wqs[:], T.ws[:], [], ["wq"])
    dma("s", "dv", T.vt[:], T.v[:], [], ["vt"])

    def step(k):
        c = {}
        for f, q0, nb in HALVES:
            z, zp = f + str(k % 2), f + str(1 - k % 2)
            gs, xg, xs, cm, cs, dd, ln, oa, lu = [T[n + z] for n in "gs xg xs cm cs dd lk oa lu".split()]
            w, ws = 16 * nb, 384 * k
            if k == 0:
                src, ak, oa, oak, st = T.ab0, "ab0", T["oz" + f], ["oz%s%d" % (f, i) for i in range(2)], 1
                ac, bc, lkk = [q0 + i for i in range(nb)], [3 + q0 + i for i in range(nb)], ["lk00", "lk01"]
                l, kk = T.lk0[:, q0:q0 + nb], T.lk0[:, 3 + q0:3 + q0 + nb]
            else:
                src, ak, oak, st = T["xs" + zp], "xs" + zp, ["oa" + z], 16
                ac, bc = [15 + 16 * i for i in range(nb)], [15 + 16 * (nb + i) for i in range(nb)]
                l, kk, lkk = T["lk" + zp][:, 0:nb], T["lk" + zp][:, nb:2 * nb], ["lk%s_%d" % (zp, i) for i in range(2 * nb)]
                c["oa" + f] = lambda oa=oa, x=src[:, 15:2 * w:16], r=ak, o=oak: cp(oa[:], x, [r], o)
            a, b = src[:, ac[0]:ac[-1] + 1:st], src[:, bc[0]:bc[-1] + 1:st]

            def d(i, nb=nb, dd=dd):
                return dd[:, i * nb:i * nb + nb]
            c["sg" + f] = lambda gs=gs, w=w, oa=oa, nb=nb, o=oak, z=z: tt(gs[:], T.sw[:, ws:ws + 384].indirect(oa[:, 0:2 * nb]), T.mk1[:, 48 - w:48 + w], A.min, o + ["sw%da" % k, "sw%db" % k, "mk1a", "mk1b"], ["gs" + z])
            c["da" + f] = lambda d=d, a=a, l=l, r=[ak] + lkk, z=z: tt(d(0), a, l, A.subtract, r, ["da" + z])
            c["db" + f] = lambda d=d, b=b, kk=kk, r=[ak] + lkk, z=z: tt(d(1), kk, b, A.subtract, r, ["db" + z])
            c["dc" + f] = lambda d=d, a=a, b=b, r=[ak], z=z: tt(d(2), a, b, A.subtract, r, ["dc" + z])
            c["bb" + f] = lambda d=d, b=b, r=[ak], z=z: ts(r, ["bb" + z], d(3), b, 384.0, None, A.add)
            c["cm" + f] = lambda cm=cm, gs=gs, w=w, z=z: tt(cm[:], gs[:, 0:w], gs[:, w:2 * w], A.is_le, ["gs" + z], ["cm" + z])
            c["sc" + f] = lambda cs=cs, cm=cm, w=w, z=z: scan(cs[:], cm[:], w, ["cm" + z], ["cs" + z])

            def sel(cs=cs, dd=dd, nb=nb, lu=lu, z=z, src=src, bc=bc, lkk=lkk, q0=q0, ak=ak, zp=zp):
                for i in range(nb):
                    cq = cs[:, 16 * i + 15:16 * i + 16]
                    lq = T.lk0[:, q0 + i:q0 + i + 1] if k == 0 else T["lk" + zp][:, i:i + 1]
                    if k < 7:
                        ts(["cs" + z, "da" + z] + lkk, ["lu%s_%d" % (z, i)], lu[:, i:i + 1], cq, dd[:, i:i + 1], lq, A.mult, A.add)
                        ts(["cs" + z, "db" + z, "bb" + z], ["lu%s_%d" % (z, nb + i)], lu[:, nb + i:nb + i + 1], cq, dd[:, nb + i:nb + i + 1], dd[:, 3 * nb + i:3 * nb + i + 1], A.mult, A.add)
                    else:
                        ts(["cs" + z, "dc" + z, ak], ["n87_%d" % (q0 + i)], T.n8[:, 21 + q0 + i:22 + q0 + i], cq, dd[:, 2 * nb + i:2 * nb + i + 1], src[:, bc[i]:bc[i] + 1], A.mult, A.add)
            c["se" + f] = sel
            c["xg" + f] = lambda xg=xg, lu=lu, w=w, nb=nb, z=z: tt(xg[:], T.tb[:, 2 * ws + 768:2 * ws + 1536].indirect(lu[:, 0:2 * nb]), T.mki[:, 0:2 * w], A.min, ["lu%s_%d" % (z, i) for i in range(2 * nb)] + ["tb%d" % (k + 1), "mki"], ["xg" + z])
            c["xs" + f] = lambda xs=xs, xg=xg, w=w, z=z: scan(xs[:], xg[:], 2 * w, ["xg" + z], ["xs" + z])

            def ends(m, cs=cs, dd=dd, nb=nb, ln=ln, z=z, src=src, bc=bc, lkk=lkk, q0=q0, ak=ak, zp=zp):
                for i in range(nb):
                    lq = T.lk0[:, q0 + i:q0 + i + 1] if k == 0 else T["lk" + zp][:, i:i + 1]
                    out, key = (T.n8[:, 3 * k + q0 + i:3 * k + q0 + i + 1], "n8%d_%d" % (k, q0 + i)) if m == 2 else (ln[:, nb * m + i:nb * m + i + 1], "lk%s_%d" % (z, nb * m + i))
                    act(out, cs[:, 16 * i + 15:16 * i + 16], F.Identity, ["cs" + z, "d" + "abc"[m] + z, ak] + lkk, [key],
                        bias=src[:, bc[i]:bc[i] + 1] if m else lq, scale=dd[:, m * nb + i:m * nb + i + 1])
            c["en" + f] = ends
        order = "sgA sgB daA dbA cmA cmB bbA dcA scA scB daB dbB bbB seA seB dcB xgA xgB xsA xsB" if k < 7 else "sgA sgB dcA dcB cmA cmB scA scB seA seB"
        for n in (("oaA oaB " if k else "") + order).split():
            c[n]()
        if k < 7:
            for m in range(3):
                for f, q0, nb in HALVES:
                    c["en" + f](m)

    for t in range(R):
        for k in range(8):
            mm(k, C, "ur", 128 * k, "qx", 96, ["ur", "urs", "qa", "qb"])
            act(T.sw[:, 384 * k:384 * k + 288], bank(k), F.Abs, ["pb%d" % k], ["sw%da" % k])
        for b in B4:
            mm(b, C, "eq", 128 * b, "qx", 96, ["eq%d" % b, "qa", "qb"])
            cp(T.vp[:, 384 * b:384 * b + 288], bank(b), ["pb%d" % b], ["vp%da" % b])
        for k in range(8):
            mm(k, 128, "ur", 128 * k, "qx", 352, ["ur", "urs", "qb", "qr"])
            act(T.sw[:, 384 * k + 288:384 * k + 384], bank(k, 96, 32), F.Abs, ["pb%d" % k], ["sw%db" % k])
        for b in B4:
            mm(b, 128, "eq", 128 * b, "qx", 352, ["eq%d" % b, "qb", "qr"])
        for k in range(8):
            step(k)
            if 1 <= k <= 4:
                act(T.vp[:, 384 * k - 96:384 * k], bank(k - 1, 96, 32), F.Copy, ["pb%d" % (k - 1)], ["vp%db" % (k - 1)])
            if k == 0:
                need("y", [], ["off"])
                wr["off"], rd["off"] = [], []
            for h in range(6):
                dma("s" if k == 7 and h > 2 else "y", "dn", T.off[16 * k:16 * k + 16, 3 * h:3 * h + 3], T.n8[16 * h:16 * h + 16, 3 * k:3 * k + 3], ["n8%d_%d" % (k, q) for q in range(3)], ["off"])
        for i in range(3):
            fill(T["inv%d" % i][:], 288.0, ["inv%d" % i])
        cp(T.nu[:], T.off[:], ["off"], ["nu"])
        cp(T.nx[:, 0:288:16], T.off[:], ["off"], ["nx"])
        for b in B4:
            w, rds = T.vp[:, 384 * b:384 * b + 384].indirect(T.nu[:, 0:18]), ["nu", "vp%da" % b, "vp%db" % b]
            if b < 2:
                act(T.mt[:, b:1152:4], w, F.Copy, rds, ["mt%d" % b])
            else:
                cp(T.mt[:, b:1152:4], w, rds, ["mt%d" % b])
            if b == 2:
                scan(T.ny[:], T.nx[:], 288, ["nx"], ["ny"])
        quant("mq", 0, 288, "mt", 0, each("mt%d"), ["mq"])
        for b in B4:
            mm(b, C, "wq", 128 * b, "mq", 0, ["wq", "mq"])
            act(T.tt[:, b:1152:4], bank(b), F.Copy, ["pb%d" % b], ["tt%d" % b], scale=0.03125)
        for b in B4:
            mm(4 + b, C, "eq", 128 * b, "qx", 96, ["eq%d" % b, "qa", "qb"])
        tt(T.nf[:], T.idt[:, 0:400].indirect(T.nu[:, 0:18]), T.mk2[:], A.min, ["idt", "nu", "mk2"], ["nf"])
        tt(T.ne[:], T.nf[:], T.ny[:], A.is_equal, ["nf", "ny"], ["ne"])
        scan(T.nz[:], T.ne[:], 288, ["ne"], ["nz"])
        ts(["nz", "rd"], ["dm"], T.dm[:], T.nz[:, 15:288:16], 0.0, T.rd[:, 0:1], A.is_gt, A.mult)
        tt(T.dn[:], T.dm[:], T.off[:], A.max, ["dm", "off"], ["dn"])
        quant("tq", 0, 288, "tt", 0, each("tt%d"), ["tq"])
        cp(T.du[:, 0:36:2], T.dn[:], ["dn"], ["du"])
        for b in B4:
            mm(b, C, "eq", 128 * b, "tq", 0, ["eq%d" % b, "tq"])
            act(T.dp[:, 304 * b:304 * b + 288], bank(b), F.Copy, ["pb%d" % b], ["dp%d" % b])
        for q in range(17, -1, -1):
            n = "inv%d" % (q % 3)
            cp(T[n][:, 0:400].indirect(T.du[:, 2 * q:2 * q + 1]), T.idt[:, 16 * q:16 * q + 16], ["du", "idt"], [n])

        def ext(n, i):
            a, b = (288, 384) if n == "b" else (0, 288)
            if i == 0:
                tt(T.inn[:, a:b], T.inv0[:, a:b], T.inv1[:, a:b], A.min, ["inv0", "inv1"], ["inn" + n])
            elif i == 1:
                tt(T.inp[:, a:b], T.inn[:, a:b], T.inv2[:, a:b], A.min, ["inn" + n, "inv2"], ["inp" + n])
            elif i == 2:
                tt(T.inm[:, a:b], T.inp[:, a:b], T.md[:, a:b], A.mult, ["inp" + n, "md"], ["inm" + n])
            elif i == 3:
                scan(T.ins[:, a:b], T.inm[:, a:b], b - a, ["inm" + n], ["ins" + n])
            else:
                cp(T.iu[:, a // 16:b // 16], T.ins[:, a + 15:b:16], ["ins" + n], ["iu" + n])
        for s in "b0 o0 b1 b2 b3 b4 o1".split():
            ext(s[0], int(s[1]))
        for b in B4:
            w, rds = T.dp[:, 304 * b:304 * b + 304].indirect(T.iu[:, 18:24]), ["iub", "dp%d" % b, "dpz%d" % b]
            if b < 2:
                act(T.ub[:, b:384:4], w, F.Copy, rds, ["ub%d" % b])
            else:
                cp(T.ub[:, b:384:4], w, rds, ["ub%d" % b])
        quant("bq", 0, 128, "ub", 0, each("ub%d") + ["ubz"], ["bq"])
        send(nxt, "ret", "rl", "qx", 0, "bq", 0, ["bq"])
        arrive("ret", prv, "qt")
        for i in (2, 3, 4):
            ext("o", i)
        for b in B4:
            w, rds, o = T.dp[:, 304 * b:304 * b + 304].indirect(T.iu[:, 0:18]), ["iuo", "dp%d" % b, "dpz%d" % b], T.uo[:, 288 * b:288 * b + 288]
            if b % 2 == 0:
                act(o, w, F.Copy, rds, ["uo%d" % b])
            else:
                cp(o, w, rds, ["uo%d" % b])
        for b in (1, 0, 3, 2):
            rds = ["pb%d" % (4 + b), "uo%d" % b]
            tt(T.xf[:, 96 * b:96 * b + 96], bank(4 + b, 96), T.uo[:, 288 * b:288 * b + 96], A.subtract, rds, ["xf%d" % b])
            tt(T.xt[:, 384 + b:1152:4], bank(4 + b, 192, 96), T.uo[:, 288 * b + 96:288 * b + 288], A.subtract, rds, ["xtb%d" % b])
        quant("qx", 224, 384, "xt", 512, each("xtb%d"), ["qb"])
        for b in B4:
            mm(b, 128, "eq", 128 * b, "qx", 0, ["eq%d" % b, "qa", "qt"])
            tt(T.xt[:, b:384:4], T.xf[:, 96 * b:96 * b + 96], bank(b, 96), A.subtract, ["xf%d" % b, "pb%d" % b], ["xta%d" % b])
        quant("qx", 96, 224, "xt", 0, each("xta%d") + each("xtb%d"), ["qa"])
        if t < R - 1:
            send_border()
    act(T.no[:], T.idt[:, 0:400].indirect(T.nu[:, 0:18]), F.Copy, ["nu", "idt"], ["no"])
    quant("vq", 0, 128, "vt", 0, ["vt"], ["vq"])
    for k in range(8):
        dma("y", "do", T.on[k:k + 1, :], T.no[16 * k:16 * k + 1, :], ["no"], ["o"])
    mm(0, C, "vq", 0, "qx", 96, ["vq", "qa", "qb"])
    dma("y", "do", T.oc[:], T.qx[:, 96:384].bitcast(dt.uint8), ["qa", "qb"], ["o"])
    for k in B4:
        dma("y", "do", T.osc[4 * k:4 * k + 4, :], T.qxs[32 * k:32 * k + 4, 96:384], ["qa", "qb"], ["o"])
    act(T.yo[:], bank(0), F.Copy, ["pb0"], ["yo"])
    dma("s", "do", T.y[:], T.yo[:], ["yo"], ["o"])
    for n in SEMAPHORES:
        if total[n]:
            learn("g", n, total[n])
